import numpy as np
import ml_dtypes


def mxq(x, axis, fmt="e4m3"):
    dtype, down = {"e4m3": (ml_dtypes.float8_e4m3fn, 7), "e5m2": (ml_dtypes.float8_e5m2, 14)}[fmt]
    v = np.moveaxis(np.asarray(x, np.float32).astype(ml_dtypes.bfloat16).astype(np.float64), axis, -1)
    blocks = v.reshape(v.shape[:-1] + (-1, 32))
    amax = np.abs(blocks).max(-1, keepdims=True)
    byte = np.maximum(np.where(amax > 0, np.frexp(amax)[1] - 1 + 127, 0) - down, 1)
    scale = np.exp2(byte - 127.0)
    codes = (blocks / scale).astype(np.float32).astype(dtype).astype(np.float64)
    return np.moveaxis((codes * scale).reshape(v.shape), -1, axis)


WIDE = False


def mx_kscale(k):
    if not WIDE:
        return np.ones(k)
    levels = np.array([10, -10, 5, -5, 0])
    if k % 512:
        return np.exp2(np.random.permutation(np.resize(levels, k // 32))).repeat(32)
    a = np.empty((k // 512, 16))
    for p in range(k // 512):
        a[p, :8] = np.random.permutation(np.resize(levels, 8))
        for g in range(8):
            far = levels[np.abs(levels - a[p, g]) >= 10]
            a[p, g + 8] = far[np.random.randint(len(far))]
    return np.exp2(a.ravel()).repeat(32)


def f64(x):
    return np.asarray(x).astype(np.float64)


def striped(idx):
    return np.tile(idx.reshape(-1, 16).T, (8, 1)).astype(np.uint16)


def unstriped(offs):
    return offs[:16].T.reshape(-1).astype(np.int64)


def pack_weight(w):
    k, n = w.shape
    w = f64(np.asarray(w, np.float32).astype(ml_dtypes.bfloat16)).reshape(k // 32, 32, n)
    amax = np.abs(w).max(1)
    byte = np.clip(np.where(amax > 0, np.frexp(amax)[1] - 1 + 127 - 7, 1), 1, 254)
    scaled = (w * np.exp2(127.0 - byte)[:, None, :]).reshape(k, n).astype(np.float32)
    words = np.ascontiguousarray(scaled.reshape(k // 512, 128, 4, n).transpose(0, 1, 3, 2)).astype(ml_dtypes.float8_e4m3fn).view(np.uint8)
    return words, np.ascontiguousarray(byte.astype(np.uint8).reshape(k // 512, 16, n))


def unpack_weight(words, scales):
    g, p, n, _ = words.shape
    vals = np.ascontiguousarray(words).view(ml_dtypes.float8_e4m3fn).astype(np.float64) * np.repeat(np.exp2(scales.astype(np.float64) - 127.0), 8, axis=1)[..., None]
    return vals.transpose(0, 1, 3, 2).reshape(g * 512, n)

def planes(y):
    n, m = y.shape
    v = y.astype(np.float32).astype(ml_dtypes.bfloat16).astype(np.float64).reshape(n // 32, 32, m)
    top = np.abs(v).max(1)
    byte = np.clip(np.where(top > 0, np.frexp(top)[1] - 1 + 127 - 7, 1), 1, 254)
    codes = (v * np.exp2(127.0 - byte)[:, None, :]).reshape(n, m).astype(np.float32).astype(ml_dtypes.float8_e4m3fn).view(np.uint8)
    words = codes.reshape(n // 512, 128, 4, m).transpose(0, 1, 3, 2)
    return np.ascontiguousarray(words), np.ascontiguousarray(byte.astype(np.uint8).reshape(n // 512, 16, m))


K, T, S, N, U = 512, 2048, 512, 512, 1024


def setup_inputs():
    n = np.random.standard_normal
    s = mx_kscale(K)[:, None]
    packed_xT = pack_weight(n((K, T)) * s)
    return {
        "x_words": packed_xT[0],
        "x_scales": packed_xT[1],
        "w1": (n((K, N)) / np.sqrt(K) / s).astype(np.float32),
        "scale": np.random.uniform(0.5, 1.5, (N, U)).astype(np.float32),
        "offs": striped(np.random.permutation(T)[:S]),
        "task": striped(np.random.permutation(U)[(U * np.random.uniform(0, 1, S) ** 4).astype(np.int64)]),
    }


def reference(x_words, x_scales, w1, scale, offs, task):
    xq = unpack_weight(x_words, x_scales)[:, unstriped(offs)]
    y = mxq(f64(w1), 0, "e4m3").T @ xq
    g = f64(scale)[:, unstriped(task)]
    out_0 = y * g
    return (out_0,) + planes(out_0)

@@ -1,0 +1,135 @@
+from contextlib import ExitStack
+
+import concourse.mybir as mybir
+
+K, T, S, N, U = 512, 2048, 512, 512, 1024
+FLOPS = 2 * K * N * S
+
+F32 = mybir.dt.float32
+BF16 = mybir.dt.bfloat16
+I32 = mybir.dt.int32
+U32 = mybir.dt.uint32
+U16 = mybir.dt.uint16
+U8 = mybir.dt.uint8
+FP8X4 = mybir.dt.float8_e4m3fn_x4
+MULT = mybir.AluOpType.mult
+
+P = 128
+PACK = 4
+HALF = S // 2
+PER_COL = 16
+
+
+def tile_picked_none_po_kernel(
+    tc, x_words, x_scales, w1, scale, offs, task, out_0, out_1, out_2
+):
+    nc = tc.nc
+    with ExitStack() as ctx:
+        lists = ctx.enter_context(tc.tile_pool(name="lists", bufs=1))
+        sb = ctx.enter_context(tc.tile_pool(name="sb", bufs=1))
+        psum = ctx.enter_context(tc.psum_pool(name="psum", bufs=1))
+
+        offs_sb = lists.tile([P, S // PER_COL], U16, name="offs_sb")
+        task_sb = lists.tile([P, S // PER_COL], U16, name="task_sb")
+        w_raw = sb.tile([P, PACK, N], F32, name="w_raw", align_bytes=64)
+        x_table = sb.tile([P, T], I32, name="x_table", align_bytes=64)
+        xs_table = sb.tile([P, T], U8, name="xs_table", align_bytes=64)
+        scale_rows = [sb.tile([P, U], F32, name=f"scale_rows{t}", align_bytes=64) for t in range(PACK)]
+
+        nc.vector.memset(xs_table[:].bitcast(I32), 0)
+        nc.sync.dma_start(offs_sb[:], offs)
+        nc.sync.dma_start(w_raw[:], w1.rearrange("(p j) m -> p j m", j=PACK))
+        for q in range(4):
+            nc.scalar.dma_start(
+                xs_table[32 * q : 32 * q + 4, :].bitcast(I32), x_scales[0, 4 * q : 4 * q + 4, :].bitcast(I32)
+            )
+        nc.sync.dma_start(x_table[:], x_words[0].rearrange("p c r -> p (c r)").bitcast(I32))
+        nc.sync.dma_start(task_sb[:], task)
+        scale_dealt = scale.rearrange("(p t) u -> p t u", t=PACK)
+        for t in range(PACK):
+            nc.sync.dma_start(scale_rows[t][:], scale_dealt[:, t, :])
+
+        xs_picked = sb.tile([P, S], U8, name="xs_picked", align_bytes=64)
+        nc.vector.tensor_copy(xs_picked[:], xs_table[:].indirect(offs_sb[:]))
+
+        w_bf = sb.tile([P, PACK, P, PACK], BF16, name="w_bf", align_bytes=64)
+        w_src = w_raw[:].rearrange("p j (m t) -> p m t j", t=PACK)
+        w_dst = w_bf[:].rearrange("p t m j -> p m t j")
+        nc.vector.tensor_copy(w_dst[:, 0:80], w_src[:, 0:80])
+        nc.scalar.copy(w_dst[:, 80:P], w_src[:, 80:P])
+        w_codes = sb.tile([P, N], U32, name="w_codes", align_bytes=64)
+        w_scales = sb.tile([P, N], U8, name="w_scales", align_bytes=64)
+        nc.vector.quantize_mx(
+            out=w_codes[:].bitcast(FP8X4), scales=w_scales[:], in_=w_bf[:].rearrange("p t m j -> p (t m j)")
+        )
+
+        x_picked = sb.tile([P, S], U32, name="x_picked", align_bytes=64)
+        for h in range(2):
+            cols = slice(h * HALF, (h + 1) * HALF)
+            lcols = slice(h * HALF // PER_COL, (h + 1) * HALF // PER_COL)
+            nc.vector.tensor_copy(x_picked[:, cols], x_table[:].bitcast(U32).indirect(offs_sb[:, lcols]))
+
+        prod = [sb.tile([P, S], F32, name=f"prod{t}", align_bytes=64) for t in range(PACK)]
+
+        def product(t, cols):
+            width = cols.stop - cols.start
+            acc = psum.tile([P, width], F32, name=f"acc{t}_{cols.start}")
+            wc = slice(t * P, (t + 1) * P)
+            nc.tensor.matmul_mx(
+                out=acc[:],
+                lhsT=w_codes[:, wc].bitcast(FP8X4),
+                lhsT_scale=w_scales[:, wc],
+                rhs=x_picked[:, cols].bitcast(FP8X4),
+                rhs_scale=xs_picked[:, cols],
+                start=True,
+                stop=True,
+            )
+            nc.scalar.copy(prod[t][:, cols], acc[:])
+
+        first, second, whole = slice(0, HALF), slice(HALF, S), slice(0, S)
+        product(0, first)
+        product(1, first)
+        product(0, second)
+        product(1, second)
+        product(2, whole)
+        product(3, whole)
+
+        y = sb.tile([P, PACK, S], F32, name="y", align_bytes=64)
+        out_dealt = out_0.rearrange("(p t) s -> p t s", t=PACK)
+
+        def scaled(t, cols):
+            lcols = slice(cols.start // PER_COL, cols.stop // PER_COL)
+            nc.vector.tensor_tensor(
+                y[:, t, cols], scale_rows[t][:].indirect(task_sb[:, lcols]), prod[t][:, cols], MULT
+            )
+
+        for t in range(PACK):
+            if t in (0, PACK - 1):
+                scaled(t, first)
+                scaled(t, second)
+            else:
+                scaled(t, whole)
+            nc.sync.dma_start(out_dealt[:, t, :], y[:, t, :])
+
+        y_codes = sb.tile([P, S], I32, name="y_codes", align_bytes=64)
+        y_scales = sb.tile([P, S], U8, name="y_scales", align_bytes=64)
+        words_out = out_1[0].rearrange("p c r -> p (c r)").bitcast(I32)
+        y_bf = [sb.tile([P, HALF, PACK], BF16, name=f"y_bf{h}", align_bytes=64) for h in range(2)]
+        nc.scalar.copy(
+            y_bf[0][:].rearrange("p (c i) t -> p c t i", i=4), y[:, :, first].rearrange("p t (c i) -> p c t i", i=4)
+        )
+        nc.vector.tensor_copy(
+            y_bf[1][:].rearrange("p (c i) t -> p c t i", i=4), y[:, :, second].rearrange("p t (c i) -> p c t i", i=4)
+        )
+        for h, cols in enumerate((first, second)):
+            nc.vector.quantize_mx(
+                out=y_codes[:, cols].bitcast(FP8X4),
+                scales=y_scales[:, cols],
+                in_=y_bf[h][:].rearrange("p c t -> p (c t)"),
+            )
+            nc.sync.dma_start(words_out[:, cols], y_codes[:, cols])
+        for q in range(4):
+            eng = nc.sync if q % 2 else nc.scalar
+            eng.dma_start(
+                out_2[0, 4 * q : 4 * q + 4, :].bitcast(I32), y_scales[32 * q : 32 * q + 4, :].bitcast(I32)
+            )

@@ -40,7 +40,7 @@ def tile_picked_none_po_kernel(
         nc.sync.dma_start(offs_sb[:], offs)
         nc.sync.dma_start(w_raw[:], w1.rearrange("(p j) m -> p j m", j=PACK))
         for q in range(4):
-            nc.scalar.dma_start(
+            nc.sync.dma_start(
                 xs_table[32 * q : 32 * q + 4, :].bitcast(I32), x_scales[0, 4 * q : 4 * q + 4, :].bitcast(I32)
             )
         nc.sync.dma_start(x_table[:], x_words[0].rearrange("p c r -> p (c r)").bitcast(I32))
@@ -55,8 +55,8 @@ def tile_picked_none_po_kernel(
         w_bf = sb.tile([P, PACK, P, PACK], BF16, name="w_bf", align_bytes=64)
         w_src = w_raw[:].rearrange("p j (m t) -> p m t j", t=PACK)
         w_dst = w_bf[:].rearrange("p t m j -> p m t j")
-        nc.vector.tensor_copy(w_dst[:, 0:80], w_src[:, 0:80])
-        nc.scalar.copy(w_dst[:, 80:P], w_src[:, 80:P])
+        nc.vector.tensor_copy(w_dst[:, 0:44], w_src[:, 0:44])
+        nc.scalar.copy(w_dst[:, 44:P], w_src[:, 44:P])
         w_codes = sb.tile([P, N], U32, name="w_codes", align_bytes=64)
         w_scales = sb.tile([P, N], U8, name="w_scales", align_bytes=64)
         nc.vector.quantize_mx(
@@ -69,11 +69,13 @@ def tile_picked_none_po_kernel(
             lcols = slice(h * HALF // PER_COL, (h + 1) * HALF // PER_COL)
             nc.vector.tensor_copy(x_picked[:, cols], x_table[:].bitcast(U32).indirect(offs_sb[:, lcols]))
 
-        prod = [sb.tile([P, S], F32, name=f"prod{t}", align_bytes=64) for t in range(PACK)]
+        out_dealt = out_0.rearrange("(p t) s -> p t s", t=PACK)
+        EARLY = 384
+        first, second = slice(0, HALF), slice(HALF, S)
+        third, early, late = slice(HALF, EARLY), slice(0, EARLY), slice(EARLY, S)
 
         def product(t, cols):
-            width = cols.stop - cols.start
-            acc = psum.tile([P, width], F32, name=f"acc{t}_{cols.start}")
+            acc = psum.tile([P, cols.stop - cols.start], F32, name=f"acc{t}_{cols.start}")
             wc = slice(t * P, (t + 1) * P)
             nc.tensor.matmul_mx(
                 out=acc[:],
@@ -84,50 +86,59 @@ def tile_picked_none_po_kernel(
                 start=True,
                 stop=True,
             )
-            nc.scalar.copy(prod[t][:, cols], acc[:])
+            return acc
 
-        first, second, whole = slice(0, HALF), slice(HALF, S), slice(0, S)
-        product(0, first)
-        product(1, first)
-        product(0, second)
-        product(1, second)
-        product(2, whole)
-        product(3, whole)
+        def entries(cols):
+            return task_sb[:, cols.start // PER_COL : cols.stop // PER_COL]
 
-        y = sb.tile([P, PACK, S], F32, name="y", align_bytes=64)
-        out_dealt = out_0.rearrange("(p t) s -> p t s", t=PACK)
+        prod = [sb.tile([P, S], F32, name=f"prod{t}", align_bytes=64) for t in range(PACK - 1)]
+        prod3_early = sb.tile([P, EARLY], F32, name="prod3_early", tag="shared", align_bytes=64)
+        prod3_late = sb.tile([P, S - EARLY], F32, name="prod3_late", align_bytes=64)
+        acc00 = product(0, first)
+        for t, cols in ((1, first), (0, second), (1, second), (2, slice(0, S))):
+            nc.scalar.copy(prod[t][:, cols], product(t, cols)[:])
+        acc3 = product(3, slice(0, S))
+        nc.scalar.copy(prod3_early[:], acc3[:, early])
+        nc.scalar.copy(prod3_late[:], acc3[:, late])
 
-        def scaled(t, cols):
-            lcols = slice(cols.start // PER_COL, cols.stop // PER_COL)
-            nc.vector.tensor_tensor(
-                y[:, t, cols], scale_rows[t][:].indirect(task_sb[:, lcols]), prod[t][:, cols], MULT
-            )
+        y_early = sb.tile([P, PACK, EARLY], F32, name="y_early", align_bytes=64)
+        g00 = sb.tile([P, HALF], F32, name="g00", align_bytes=64)
+        nc.vector.tensor_copy(g00[:], scale_rows[0][:].indirect(entries(first)))
+        nc.vector.tensor_tensor(y_early[:, 0, first], acc00[:], g00[:], MULT)
 
+        def scaled(dst, t, cols, src):
+            nc.vector.tensor_tensor(dst, scale_rows[t][:].indirect(entries(cols)), src, MULT)
+
+        scaled(y_early[:, 0, third], 0, third, prod[0][:, third])
+        nc.sync.dma_start(out_dealt[:, 0, early], y_early[:, 0, :])
+        for t in (1, 2):
+            scaled(y_early[:, t, :], t, early, prod[t][:, early])
+            nc.sync.dma_start(out_dealt[:, t, early], y_early[:, t, :])
+        for cols in (first, third):
+            scaled(y_early[:, 3, cols], 3, cols, prod3_early[:, cols])
+        nc.sync.dma_start(out_dealt[:, 3, early], y_early[:, 3, :])
+
+        y_late = sb.tile([P, PACK, S - EARLY], F32, name="y_late", tag="shared", align_bytes=64)
         for t in range(PACK):
-            if t in (0, PACK - 1):
-                scaled(t, first)
-                scaled(t, second)
-            else:
-                scaled(t, whole)
-            nc.sync.dma_start(out_dealt[:, t, :], y[:, t, :])
+            scaled(y_late[:, t, :], t, late, prod[t][:, late] if t < PACK - 1 else prod3_late[:])
+        nc.sync.dma_start(out_dealt[:, :, late], y_late[:])
 
         y_codes = sb.tile([P, S], I32, name="y_codes", align_bytes=64)
         y_scales = sb.tile([P, S], U8, name="y_scales", align_bytes=64)
         words_out = out_1[0].rearrange("p c r -> p (c r)").bitcast(I32)
-        y_bf = [sb.tile([P, HALF, PACK], BF16, name=f"y_bf{h}", align_bytes=64) for h in range(2)]
-        nc.scalar.copy(
-            y_bf[0][:].rearrange("p (c i) t -> p c t i", i=4), y[:, :, first].rearrange("p t (c i) -> p c t i", i=4)
-        )
-        nc.vector.tensor_copy(
-            y_bf[1][:].rearrange("p (c i) t -> p c t i", i=4), y[:, :, second].rearrange("p t (c i) -> p c t i", i=4)
-        )
-        for h, cols in enumerate((first, second)):
+        pieces = ((first, y_early[:, :, first]), (third, y_early[:, :, third]), (late, y_late[:]))
+        for cols, src in pieces:
+            y_bf = sb.tile([P, cols.stop - cols.start, PACK], BF16, name=f"y_bf{cols.start}", align_bytes=64)
+            cast = nc.vector.tensor_copy if cols.start == EARLY else nc.scalar.copy
+            cast(y_bf[:].rearrange("p (c i) t -> p c t i", i=4), src.rearrange("p t (c i) -> p c t i", i=4))
             nc.vector.quantize_mx(
                 out=y_codes[:, cols].bitcast(FP8X4),
                 scales=y_scales[:, cols],
-                in_=y_bf[h][:].rearrange("p c t -> p (c t)"),
+                in_=y_bf[:].rearrange("p c t -> p (c t)"),
             )
-            nc.sync.dma_start(words_out[:, cols], y_codes[:, cols])
+            if cols.start == HALF:
+                nc.sync.dma_start(words_out[:, early], y_codes[:, early])
+        nc.sync.dma_start(words_out[:, late], y_codes[:, late])
         for q in range(4):
             eng = nc.sync if q % 2 else nc.scalar
             eng.dma_start(

@@ -37,12 +37,11 @@ def tile_picked_none_po_kernel(
         scale_rows = [sb.tile([P, U], F32, name=f"scale_rows{t}", align_bytes=64) for t in range(PACK)]
 
         nc.vector.memset(xs_table[:].bitcast(I32), 0)
-        nc.sync.dma_start(offs_sb[:], offs)
         nc.sync.dma_start(w_raw[:], w1.rearrange("(p j) m -> p j m", j=PACK))
-        for q in range(4):
-            nc.sync.dma_start(
-                xs_table[32 * q : 32 * q + 4, :].bitcast(I32), x_scales[0, 4 * q : 4 * q + 4, :].bitcast(I32)
-            )
+        nc.sync.dma_start(offs_sb[:], offs)
+        xs_rows = x_scales[0].rearrange("(q r) c -> r q c", r=4)
+        for r in range(4):
+            nc.sync.dma_start(xs_table[r:P:32, :].bitcast(I32), xs_rows[r].bitcast(I32))
         nc.sync.dma_start(x_table[:], x_words[0].rearrange("p c r -> p (c r)").bitcast(I32))
         nc.sync.dma_start(task_sb[:], task)
         scale_dealt = scale.rearrange("(p t) u -> p t u", t=PACK)
@@ -55,8 +54,8 @@ def tile_picked_none_po_kernel(
         w_bf = sb.tile([P, PACK, P, PACK], BF16, name="w_bf", align_bytes=64)
         w_src = w_raw[:].rearrange("p j (m t) -> p m t j", t=PACK)
         w_dst = w_bf[:].rearrange("p t m j -> p m t j")
-        nc.vector.tensor_copy(w_dst[:, 0:44], w_src[:, 0:44])
-        nc.scalar.copy(w_dst[:, 44:P], w_src[:, 44:P])
+        nc.vector.tensor_copy(w_dst[:, 0:52], w_src[:, 0:52])
+        nc.scalar.copy(w_dst[:, 52:P], w_src[:, 52:P])
         w_codes = sb.tile([P, N], U32, name="w_codes", align_bytes=64)
         w_scales = sb.tile([P, N], U8, name="w_scales", align_bytes=64)
         nc.vector.quantize_mx(
@@ -92,14 +91,14 @@ def tile_picked_none_po_kernel(
             return task_sb[:, cols.start // PER_COL : cols.stop // PER_COL]
 
         prod = [sb.tile([P, S], F32, name=f"prod{t}", align_bytes=64) for t in range(PACK - 1)]
-        prod3_early = sb.tile([P, EARLY], F32, name="prod3_early", tag="shared", align_bytes=64)
-        prod3_late = sb.tile([P, S - EARLY], F32, name="prod3_late", align_bytes=64)
+        prod3_first = sb.tile([P, HALF], F32, name="prod3_first", tag="shared", align_bytes=64)
+        prod3_second = sb.tile([P, HALF], F32, name="prod3_second", align_bytes=64)
         acc00 = product(0, first)
         for t, cols in ((1, first), (0, second), (1, second), (2, slice(0, S))):
             nc.scalar.copy(prod[t][:, cols], product(t, cols)[:])
         acc3 = product(3, slice(0, S))
-        nc.scalar.copy(prod3_early[:], acc3[:, early])
-        nc.scalar.copy(prod3_late[:], acc3[:, late])
+        nc.scalar.copy(prod3_first[:], acc3[:, first])
+        nc.scalar.copy(prod3_second[:], acc3[:, second])
 
         y_early = sb.tile([P, PACK, EARLY], F32, name="y_early", align_bytes=64)
         g00 = sb.tile([P, HALF], F32, name="g00", align_bytes=64)
@@ -114,33 +113,39 @@ def tile_picked_none_po_kernel(
         for t in (1, 2):
             scaled(y_early[:, t, :], t, early, prod[t][:, early])
             nc.sync.dma_start(out_dealt[:, t, early], y_early[:, t, :])
-        for cols in (first, third):
-            scaled(y_early[:, 3, cols], 3, cols, prod3_early[:, cols])
+        scaled(y_early[:, 3, first], 3, first, prod3_first[:])
+        scaled(y_early[:, 3, third], 3, third, prod3_second[:, : EARLY - HALF])
         nc.sync.dma_start(out_dealt[:, 3, early], y_early[:, 3, :])
 
         y_late = sb.tile([P, PACK, S - EARLY], F32, name="y_late", tag="shared", align_bytes=64)
         for t in range(PACK):
-            scaled(y_late[:, t, :], t, late, prod[t][:, late] if t < PACK - 1 else prod3_late[:])
-        nc.sync.dma_start(out_dealt[:, :, late], y_late[:])
+            scaled(y_late[:, t, :], t, late, prod[t][:, late] if t < PACK - 1 else prod3_second[:, EARLY - HALF :])
+            if t % 2:
+                nc.sync.dma_start(out_dealt[:, t - 1 : t + 1, late], y_late[:, t - 1 : t + 1, :])
 
         y_codes = sb.tile([P, S], I32, name="y_codes", align_bytes=64)
         y_scales = sb.tile([P, S], U8, name="y_scales", align_bytes=64)
         words_out = out_1[0].rearrange("p c r -> p (c r)").bitcast(I32)
-        pieces = ((first, y_early[:, :, first]), (third, y_early[:, :, third]), (late, y_late[:]))
-        for cols, src in pieces:
-            y_bf = sb.tile([P, cols.stop - cols.start, PACK], BF16, name=f"y_bf{cols.start}", align_bytes=64)
-            cast = nc.vector.tensor_copy if cols.start == EARLY else nc.scalar.copy
-            cast(y_bf[:].rearrange("p (c i) t -> p c t i", i=4), src.rearrange("p t (c i) -> p c t i", i=4))
+        y_bf = [sb.tile([P, HALF, PACK], BF16, name=f"y_bf{h}", align_bytes=64) for h in range(2)]
+
+        def rounded(copy, dst, src):
+            copy(dst.rearrange("p (c i) t -> p c t i", i=4), src.rearrange("p t (c i) -> p c t i", i=4))
+
+        def quantised(h, cols):
             nc.vector.quantize_mx(
                 out=y_codes[:, cols].bitcast(FP8X4),
                 scales=y_scales[:, cols],
-                in_=y_bf[:].rearrange("p c t -> p (c t)"),
+                in_=y_bf[h][:].rearrange("p c t -> p (c t)"),
             )
-            if cols.start == HALF:
-                nc.sync.dma_start(words_out[:, early], y_codes[:, early])
-        nc.sync.dma_start(words_out[:, late], y_codes[:, late])
-        for q in range(4):
-            eng = nc.sync if q % 2 else nc.scalar
-            eng.dma_start(
-                out_2[0, 4 * q : 4 * q + 4, :].bitcast(I32), y_scales[32 * q : 32 * q + 4, :].bitcast(I32)
-            )
+            nc.sync.dma_start(words_out[:, cols], y_codes[:, cols])
+
+        rounded(nc.scalar.copy, y_bf[0][:], y_early[:, :, first])
+        quantised(0, first)
+        rounded(nc.scalar.copy, y_bf[1][:, 0:128], y_early[:, :, third])
+        rounded(nc.scalar.copy, y_bf[1][:, 128:192], y_late[:, :, 0:64])
+        rounded(nc.vector.tensor_copy, y_bf[1][:, 192:256], y_late[:, :, 64:128])
+        quantised(1, second)
+        ys_rows = out_2[0].rearrange("(q r) c -> r q c", r=4)
+        for r in range(4):
+            eng = nc.sync if r % 2 else nc.scalar
+            eng.dma_start(ys_rows[r].bitcast(I32), y_scales[r:P:32, :].bitcast(I32))

@@ -17,6 +17,7 @@ MULT = mybir.AluOpType.mult
 P = 128
 PACK = 4
 HALF = S // 2
+QUARTER = S // 4
 PER_COL = 16
 
 
@@ -48,8 +49,8 @@ def tile_picked_none_po_kernel(
         for t in range(PACK):
             nc.sync.dma_start(scale_rows[t][:], scale_dealt[:, t, :])
 
-        xs_picked = sb.tile([P, S], U8, name="xs_picked", align_bytes=64)
-        nc.vector.tensor_copy(xs_picked[:], xs_table[:].indirect(offs_sb[:]))
+        xs_placed = sb.tile([P, S], U8, name="xs_placed", align_bytes=64)
+        nc.vector.tensor_copy(xs_placed[:], xs_table[:].indirect(offs_sb[:]))
 
         w_bf = sb.tile([P, PACK, P, PACK], BF16, name="w_bf", align_bytes=64)
         w_src = w_raw[:].rearrange("p j (m t) -> p m t j", t=PACK)
@@ -62,18 +63,18 @@ def tile_picked_none_po_kernel(
             out=w_codes[:].bitcast(FP8X4), scales=w_scales[:], in_=w_bf[:].rearrange("p t m j -> p (t m j)")
         )
 
+        def entries(lst, cols):
+            return lst[:, cols.start // PER_COL : cols.stop // PER_COL]
+
+        quarters = [slice(q * QUARTER, (q + 1) * QUARTER) for q in range(4)]
+        first, second, whole = slice(0, HALF), slice(HALF, S), slice(0, S)
+
         x_picked = sb.tile([P, S], U32, name="x_picked", align_bytes=64)
-        for h in range(2):
-            cols = slice(h * HALF, (h + 1) * HALF)
-            lcols = slice(h * HALF // PER_COL, (h + 1) * HALF // PER_COL)
-            nc.vector.tensor_copy(x_picked[:, cols], x_table[:].bitcast(U32).indirect(offs_sb[:, lcols]))
+        for cols in (first, second):
+            nc.vector.tensor_copy(x_picked[:, cols], x_table[:].bitcast(U32).indirect(entries(offs_sb, cols)))
 
-        out_dealt = out_0.rearrange("(p t) s -> p t s", t=PACK)
-        EARLY = 384
-        first, second = slice(0, HALF), slice(HALF, S)
-        third, early, late = slice(HALF, EARLY), slice(0, EARLY), slice(EARLY, S)
-
-        def product(t, cols):
+        prod = [sb.tile([P, S], F32, name=f"prod{t}", align_bytes=64) for t in range(PACK)]
+        for t, cols in ((0, first), (1, first), (0, second), (1, second), (2, whole), (3, whole)):
             acc = psum.tile([P, cols.stop - cols.start], F32, name=f"acc{t}_{cols.start}")
             wc = slice(t * P, (t + 1) * P)
             nc.tensor.matmul_mx(
@@ -81,55 +82,26 @@ def tile_picked_none_po_kernel(
                 lhsT=w_codes[:, wc].bitcast(FP8X4),
                 lhsT_scale=w_scales[:, wc],
                 rhs=x_picked[:, cols].bitcast(FP8X4),
-                rhs_scale=xs_picked[:, cols],
+                rhs_scale=xs_placed[:, cols],
                 start=True,
                 stop=True,
             )
-            return acc
+            nc.scalar.copy(prod[t][:, cols], acc[:])
 
-        def entries(cols):
-            return task_sb[:, cols.start // PER_COL : cols.stop // PER_COL]
-
-        prod = [sb.tile([P, S], F32, name=f"prod{t}", align_bytes=64) for t in range(PACK - 1)]
-        prod3_first = sb.tile([P, HALF], F32, name="prod3_first", tag="shared", align_bytes=64)
-        prod3_second = sb.tile([P, HALF], F32, name="prod3_second", align_bytes=64)
-        acc00 = product(0, first)
-        for t, cols in ((1, first), (0, second), (1, second), (2, slice(0, S))):
-            nc.scalar.copy(prod[t][:, cols], product(t, cols)[:])
-        acc3 = product(3, slice(0, S))
-        nc.scalar.copy(prod3_first[:], acc3[:, first])
-        nc.scalar.copy(prod3_second[:], acc3[:, second])
-
-        y_early = sb.tile([P, PACK, EARLY], F32, name="y_early", align_bytes=64)
-        g00 = sb.tile([P, HALF], F32, name="g00", align_bytes=64)
-        nc.vector.tensor_copy(g00[:], scale_rows[0][:].indirect(entries(first)))
-        nc.vector.tensor_tensor(y_early[:, 0, first], acc00[:], g00[:], MULT)
-
-        def scaled(dst, t, cols, src):
-            nc.vector.tensor_tensor(dst, scale_rows[t][:].indirect(entries(cols)), src, MULT)
-
-        scaled(y_early[:, 0, third], 0, third, prod[0][:, third])
-        nc.sync.dma_start(out_dealt[:, 0, early], y_early[:, 0, :])
-        for t in (1, 2):
-            scaled(y_early[:, t, :], t, early, prod[t][:, early])
-            nc.sync.dma_start(out_dealt[:, t, early], y_early[:, t, :])
-        scaled(y_early[:, 3, first], 3, first, prod3_first[:])
-        scaled(y_early[:, 3, third], 3, third, prod3_second[:, : EARLY - HALF])
-        nc.sync.dma_start(out_dealt[:, 3, early], y_early[:, 3, :])
-
-        y_late = sb.tile([P, PACK, S - EARLY], F32, name="y_late", tag="shared", align_bytes=64)
-        for t in range(PACK):
-            scaled(y_late[:, t, :], t, late, prod[t][:, late] if t < PACK - 1 else prod3_second[:, EARLY - HALF :])
-            if t % 2:
-                nc.sync.dma_start(out_dealt[:, t - 1 : t + 1, late], y_late[:, t - 1 : t + 1, :])
-
+        out_dealt = out_0.rearrange("(p t) s -> p t s", t=PACK)
+        y = sb.tile([P, PACK, S], F32, name="y", align_bytes=64)
+        y_bf = [sb.tile([P, HALF, PACK], BF16, name=f"y_bf{h}", align_bytes=64) for h in range(2)]
         y_codes = sb.tile([P, S], I32, name="y_codes", align_bytes=64)
         y_scales = sb.tile([P, S], U8, name="y_scales", align_bytes=64)
         words_out = out_1[0].rearrange("p c r -> p (c r)").bitcast(I32)
-        y_bf = [sb.tile([P, HALF, PACK], BF16, name=f"y_bf{h}", align_bytes=64) for h in range(2)]
 
-        def rounded(copy, dst, src):
-            copy(dst.rearrange("p (c i) t -> p c t i", i=4), src.rearrange("p t (c i) -> p c t i", i=4))
+        def scaled(t, cols):
+            nc.vector.tensor_tensor(y[:, t, cols], scale_rows[t][:].indirect(entries(task_sb, cols)), prod[t][:, cols], MULT)
+
+        def rounded(copy, planes, cols):
+            h, c0 = divmod(cols.start, HALF)
+            dst = y_bf[h][:, c0 : c0 + cols.stop - cols.start, planes]
+            copy(dst.rearrange("p (c i) t -> p c t i", i=4), y[:, planes, cols].rearrange("p t (c i) -> p c t i", i=4))
 
         def quantised(h, cols):
             nc.vector.quantize_mx(
@@ -139,11 +111,24 @@ def tile_picked_none_po_kernel(
             )
             nc.sync.dma_start(words_out[:, cols], y_codes[:, cols])
 
-        rounded(nc.scalar.copy, y_bf[0][:], y_early[:, :, first])
+        for cols in (first, second):
+            scaled(0, cols)
+        nc.sync.dma_start(out_dealt[:, 0, :], y[:, 0, :])
+        scaled(1, whole)
+        nc.sync.dma_start(out_dealt[:, 1, :], y[:, 1, :])
+        for cols in (first, second):
+            rounded(nc.scalar.copy, slice(0, 2), cols)
+        scaled(2, whole)
+        nc.sync.dma_start(out_dealt[:, 2, :], y[:, 2, :])
+        for q, cols in enumerate(quarters):
+            scaled(3, cols)
+            if q < 3:
+                rounded(nc.scalar.copy, slice(2, 4), cols)
+            if q % 2:
+                half = (first, second)[q // 2]
+                nc.sync.dma_start(out_dealt[:, 3, half], y[:, 3, half])
         quantised(0, first)
-        rounded(nc.scalar.copy, y_bf[1][:, 0:128], y_early[:, :, third])
-        rounded(nc.scalar.copy, y_bf[1][:, 128:192], y_late[:, :, 0:64])
-        rounded(nc.vector.tensor_copy, y_bf[1][:, 192:256], y_late[:, :, 64:128])
+        rounded(nc.vector.tensor_copy, slice(2, 4), quarters[3])
         quantised(1, second)
         ys_rows = out_2[0].rearrange("(q r) c -> r q c", r=4)
         for r in range(4):

@@ -73,8 +73,10 @@ def tile_picked_none_po_kernel(
         for cols in (first, second):
             nc.vector.tensor_copy(x_picked[:, cols], x_table[:].bitcast(U32).indirect(entries(offs_sb, cols)))
 
-        prod = [sb.tile([P, S], F32, name=f"prod{t}", align_bytes=64) for t in range(PACK)]
-        for t, cols in ((0, first), (1, first), (0, second), (1, second), (2, whole), (3, whole)):
+        EARLY = 384
+        early, late, third = slice(0, EARLY), slice(EARLY, S), quarters[2]
+
+        def product(t, cols):
             acc = psum.tile([P, cols.stop - cols.start], F32, name=f"acc{t}_{cols.start}")
             wc = slice(t * P, (t + 1) * P)
             nc.tensor.matmul_mx(
@@ -86,50 +88,72 @@ def tile_picked_none_po_kernel(
                 start=True,
                 stop=True,
             )
-            nc.scalar.copy(prod[t][:, cols], acc[:])
+            return acc
+
+        prod1 = sb.tile([P, S], F32, name="prod1", align_bytes=64)
+        prod2 = sb.tile([P, S], F32, name="prod2", align_bytes=64)
+        prod3_head = sb.tile([P, QUARTER], F32, name="prod3_head", tag="shared", align_bytes=64)
+        prod3 = sb.tile([P, S], F32, name="prod3", align_bytes=64)
+        acc0_first = product(0, first)
+        nc.scalar.copy(prod1[:, first], product(1, first)[:])
+        acc0_second = product(0, second)
+        nc.scalar.copy(prod1[:, second], product(1, second)[:])
+        nc.scalar.copy(prod2[:], product(2, whole)[:])
+        acc3 = product(3, whole)
+        nc.scalar.copy(prod3_head[:], acc3[:, quarters[0]])
+        nc.scalar.copy(prod3[:, QUARTER:], acc3[:, QUARTER:])
 
         out_dealt = out_0.rearrange("(p t) s -> p t s", t=PACK)
-        y = sb.tile([P, PACK, S], F32, name="y", align_bytes=64)
-        y_bf = [sb.tile([P, HALF, PACK], BF16, name=f"y_bf{h}", align_bytes=64) for h in range(2)]
+        y_early = sb.tile([P, PACK, EARLY], F32, name="y_early", align_bytes=64)
+        picked0 = sb.tile([P, S], F32, name="picked0", align_bytes=64)
+        for cols in (first, second):
+            nc.vector.tensor_copy(picked0[:, cols], scale_rows[0][:].indirect(entries(task_sb, cols)))
+        nc.vector.tensor_tensor(y_early[:, 0, first], acc0_first[:], picked0[:, first], MULT)
+        nc.vector.tensor_tensor(y_early[:, 0, third], acc0_second[:, :QUARTER], picked0[:, third], MULT)
+        nc.sync.dma_start(out_dealt[:, 0, early], y_early[:, 0, :])
+
+        def scaled(dst, t, cols, src):
+            nc.vector.tensor_tensor(dst, scale_rows[t][:].indirect(entries(task_sb, cols)), src, MULT)
+
+        for t, prod in ((1, prod1), (2, prod2)):
+            scaled(y_early[:, t, :], t, early, prod[:, early])
+            nc.sync.dma_start(out_dealt[:, t, early], y_early[:, t, :])
+        scaled(y_early[:, 3, quarters[0]], 3, quarters[0], prod3_head[:])
+        for cols in quarters[1:3]:
+            scaled(y_early[:, 3, cols], 3, cols, prod3[:, cols])
+        nc.sync.dma_start(out_dealt[:, 3, early], y_early[:, 3, :])
+
+        y_late = sb.tile([P, PACK, S - EARLY], F32, name="y_late", tag="shared", align_bytes=64)
+        nc.vector.tensor_tensor(y_late[:, 0, :], acc0_second[:, QUARTER:], picked0[:, late], MULT)
+        for t, prod in ((1, prod1), (2, prod2), (3, prod3)):
+            scaled(y_late[:, t, :], t, late, prod[:, late])
+            if t % 2:
+                nc.sync.dma_start(out_dealt[:, t - 1 : t + 1, late], y_late[:, t - 1 : t + 1, :])
+
         y_codes = sb.tile([P, S], I32, name="y_codes", align_bytes=64)
         y_scales = sb.tile([P, S], U8, name="y_scales", align_bytes=64)
         words_out = out_1[0].rearrange("p c r -> p (c r)").bitcast(I32)
+        y_bf = sb.tile([P, S, PACK], BF16, name="y_bf", align_bytes=64)
 
-        def scaled(t, cols):
-            nc.vector.tensor_tensor(y[:, t, cols], scale_rows[t][:].indirect(entries(task_sb, cols)), prod[t][:, cols], MULT)
+        def rounded(copy, cols, src):
+            copy(y_bf[:, cols].rearrange("p (c i) t -> p c t i", i=4), src.rearrange("p t (c i) -> p c t i", i=4))
 
-        def rounded(copy, planes, cols):
-            h, c0 = divmod(cols.start, HALF)
-            dst = y_bf[h][:, c0 : c0 + cols.stop - cols.start, planes]
-            copy(dst.rearrange("p (c i) t -> p c t i", i=4), y[:, planes, cols].rearrange("p t (c i) -> p c t i", i=4))
-
-        def quantised(h, cols):
+        def quantised(cols):
             nc.vector.quantize_mx(
                 out=y_codes[:, cols].bitcast(FP8X4),
                 scales=y_scales[:, cols],
-                in_=y_bf[h][:].rearrange("p c t -> p (c t)"),
+                in_=y_bf[:, cols].rearrange("p c t -> p (c t)"),
             )
-            nc.sync.dma_start(words_out[:, cols], y_codes[:, cols])
 
-        for cols in (first, second):
-            scaled(0, cols)
-        nc.sync.dma_start(out_dealt[:, 0, :], y[:, 0, :])
-        scaled(1, whole)
-        nc.sync.dma_start(out_dealt[:, 1, :], y[:, 1, :])
-        for cols in (first, second):
-            rounded(nc.scalar.copy, slice(0, 2), cols)
-        scaled(2, whole)
-        nc.sync.dma_start(out_dealt[:, 2, :], y[:, 2, :])
-        for q, cols in enumerate(quarters):
-            scaled(3, cols)
-            if q < 3:
-                rounded(nc.scalar.copy, slice(2, 4), cols)
-            if q % 2:
-                half = (first, second)[q // 2]
-                nc.sync.dma_start(out_dealt[:, 3, half], y[:, 3, half])
-        quantised(0, first)
-        rounded(nc.vector.tensor_copy, slice(2, 4), quarters[3])
-        quantised(1, second)
+        for cols in quarters[:3]:
+            rounded(nc.scalar.copy, cols, y_early[:, :, cols])
+        rounded(nc.scalar.copy, slice(EARLY, EARLY + 64), y_late[:, :, 0:64])
+        quantised(first)
+        nc.sync.dma_start(words_out[:, first], y_codes[:, first])
+        rounded(nc.vector.tensor_copy, slice(EARLY + 64, S), y_late[:, :, 64:128])
+        quantised(third)
+        quantised(late)
+        nc.sync.dma_start(words_out[:, second], y_codes[:, second])
         ys_rows = out_2[0].rearrange("(q r) c -> r q c", r=4)
         for r in range(4):
             eng = nc.sync if r % 2 else nc.scalar

@@ -32,31 +32,39 @@ def tile_picked_none_po_kernel(
 
         offs_sb = lists.tile([P, S // PER_COL], U16, name="offs_sb")
         task_sb = lists.tile([P, S // PER_COL], U16, name="task_sb")
-        w_raw = sb.tile([P, PACK, N], F32, name="w_raw", align_bytes=64)
+        turns = ctx.enter_context(tc.tile_pool(name="turns", bufs=1))
+        row_bytes = 4 * U
+        w_raw = turns.tile([P, PACK, N], F32, name="w_raw", offset=3 * row_bytes // 2)
+        xs_table = turns.tile([P, T], U8, name="xs_table", offset=0)
         x_table = sb.tile([P, T], I32, name="x_table", align_bytes=64)
-        xs_table = sb.tile([P, T], U8, name="xs_table", align_bytes=64)
-        scale_rows = [sb.tile([P, U], F32, name=f"scale_rows{t}", align_bytes=64) for t in range(PACK)]
+        xs_picked = sb.tile([P, S], U8, name="xs_picked", align_bytes=64)
+        xs_placed = sb.tile([P, S], U8, name="xs_placed", align_bytes=64)
 
         nc.vector.memset(xs_table[:].bitcast(I32), 0)
-        nc.sync.dma_start(w_raw[:], w1.rearrange("(p j) m -> p j m", j=PACK))
+        nc.vector.memset(xs_placed[:].bitcast(I32), 0)
+        x_rows = x_words[0].rearrange("p c r -> p (c r)").bitcast(I32)
+        w_dealt = w1.rearrange("(p j) m -> p j m", j=PACK)
+        nc.sync.dma_start(w_raw[:, :, : N // 4], w_dealt[:, :, : N // 4])
         nc.sync.dma_start(offs_sb[:], offs)
-        xs_rows = x_scales[0].rearrange("(q r) c -> r q c", r=4)
-        for r in range(4):
-            nc.sync.dma_start(xs_table[r:P:32, :].bitcast(I32), xs_rows[r].bitcast(I32))
-        nc.sync.dma_start(x_table[:], x_words[0].rearrange("p c r -> p (c r)").bitcast(I32))
+        nc.sync.dma_start(xs_table[0:P:8, :].bitcast(I32), x_scales[0].bitcast(I32))
+        nc.sync.dma_start(w_raw[:, :, N // 4 :], w_dealt[:, :, N // 4 :])
+        nc.sync.dma_start(x_table[:], x_rows)
         nc.sync.dma_start(task_sb[:], task)
-        scale_dealt = scale.rearrange("(p t) u -> p t u", t=PACK)
-        for t in range(PACK):
-            nc.sync.dma_start(scale_rows[t][:], scale_dealt[:, t, :])
 
-        xs_placed = sb.tile([P, S], U8, name="xs_placed", align_bytes=64)
-        nc.vector.tensor_copy(xs_placed[:], xs_table[:].indirect(offs_sb[:]))
+        nc.vector.tensor_copy(xs_picked[:], xs_table[:].indirect(offs_sb[:]))
+        for r in range(4):
+            nc.sync.dma_start(xs_placed[r:P:32, :].bitcast(I32), xs_picked[8 * r : P : 32, :].bitcast(I32))
 
         w_bf = sb.tile([P, PACK, P, PACK], BF16, name="w_bf", align_bytes=64)
         w_src = w_raw[:].rearrange("p j (m t) -> p m t j", t=PACK)
         w_dst = w_bf[:].rearrange("p t m j -> p m t j")
-        nc.vector.tensor_copy(w_dst[:, 0:52], w_src[:, 0:52])
-        nc.scalar.copy(w_dst[:, 52:P], w_src[:, 52:P])
+        nc.scalar.copy(w_dst[:, 0:32], w_src[:, 0:32])
+        nc.vector.tensor_copy(w_dst[:, 32:88], w_src[:, 32:88])
+        nc.scalar.copy(w_dst[:, 88:P], w_src[:, 88:P])
+        scale_rows = [turns.tile([P, U], F32, name=f"scale_rows{t}", offset=t * row_bytes) for t in range(PACK)]
+        scale_dealt = scale.rearrange("(p t) u -> p t u", t=PACK)
+        for t in range(PACK):
+            nc.sync.dma_start(scale_rows[t][:], scale_dealt[:, t, :])
         w_codes = sb.tile([P, N], U32, name="w_codes", align_bytes=64)
         w_scales = sb.tile([P, N], U8, name="w_scales", align_bytes=64)
         nc.vector.quantize_mx(
@@ -127,8 +135,7 @@ def tile_picked_none_po_kernel(
         nc.vector.tensor_tensor(y_late[:, 0, :], acc0_second[:, QUARTER:], picked0[:, late], MULT)
         for t, prod in ((1, prod1), (2, prod2), (3, prod3)):
             scaled(y_late[:, t, :], t, late, prod[:, late])
-            if t % 2:
-                nc.sync.dma_start(out_dealt[:, t - 1 : t + 1, late], y_late[:, t - 1 : t + 1, :])
+        nc.sync.dma_start(out_dealt[:, :, late], y_late[:])
 
         y_codes = sb.tile([P, S], I32, name="y_codes", align_bytes=64)
         y_scales = sb.tile([P, S], U8, name="y_scales", align_bytes=64)

@@ -34,7 +34,7 @@ def tile_picked_none_po_kernel(
         task_sb = lists.tile([P, S // PER_COL], U16, name="task_sb")
         turns = ctx.enter_context(tc.tile_pool(name="turns", bufs=1))
         row_bytes = 4 * U
-        w_raw = turns.tile([P, PACK, N], F32, name="w_raw", offset=3 * row_bytes // 2)
+        w_raw = turns.tile([P, PACK, N], F32, name="w_raw", offset=row_bytes)
         xs_table = turns.tile([P, T], U8, name="xs_table", offset=0)
         x_table = sb.tile([P, T], I32, name="x_table", align_bytes=64)
         xs_picked = sb.tile([P, S], U8, name="xs_picked", align_bytes=64)
@@ -44,12 +44,15 @@ def tile_picked_none_po_kernel(
         nc.vector.memset(xs_placed[:].bitcast(I32), 0)
         x_rows = x_words[0].rearrange("p c r -> p (c r)").bitcast(I32)
         w_dealt = w1.rearrange("(p j) m -> p j m", j=PACK)
-        nc.sync.dma_start(w_raw[:, :, : N // 4], w_dealt[:, :, : N // 4])
+        nc.sync.dma_start(w_raw[:, :, : N // 2], w_dealt[:, :, : N // 2])
         nc.sync.dma_start(offs_sb[:], offs)
         nc.sync.dma_start(xs_table[0:P:8, :].bitcast(I32), x_scales[0].bitcast(I32))
-        nc.sync.dma_start(w_raw[:, :, N // 4 :], w_dealt[:, :, N // 4 :])
+        nc.sync.dma_start(w_raw[:, :, N // 2 :], w_dealt[:, :, N // 2 :])
         nc.sync.dma_start(x_table[:], x_rows)
         nc.sync.dma_start(task_sb[:], task)
+        scale_dealt = scale.rearrange("(p t) u -> p t u", t=PACK)
+        scale_rows = [sb.tile([P, U], F32, name="scale_rows0", align_bytes=64)]
+        nc.sync.dma_start(scale_rows[0][:], scale_dealt[:, 0, :])
 
         nc.vector.tensor_copy(xs_picked[:], xs_table[:].indirect(offs_sb[:]))
         for r in range(4):
@@ -58,12 +61,11 @@ def tile_picked_none_po_kernel(
         w_bf = sb.tile([P, PACK, P, PACK], BF16, name="w_bf", align_bytes=64)
         w_src = w_raw[:].rearrange("p j (m t) -> p m t j", t=PACK)
         w_dst = w_bf[:].rearrange("p t m j -> p m t j")
-        nc.scalar.copy(w_dst[:, 0:32], w_src[:, 0:32])
-        nc.vector.tensor_copy(w_dst[:, 32:88], w_src[:, 32:88])
-        nc.scalar.copy(w_dst[:, 88:P], w_src[:, 88:P])
-        scale_rows = [turns.tile([P, U], F32, name=f"scale_rows{t}", offset=t * row_bytes) for t in range(PACK)]
-        scale_dealt = scale.rearrange("(p t) u -> p t u", t=PACK)
-        for t in range(PACK):
+        nc.scalar.copy(w_dst[:, 0:64], w_src[:, 0:64])
+        nc.vector.tensor_copy(w_dst[:, 64:104], w_src[:, 64:104])
+        nc.scalar.copy(w_dst[:, 104:P], w_src[:, 104:P])
+        for t in range(1, PACK):
+            scale_rows.append(turns.tile([P, U], F32, name=f"scale_rows{t}", offset=(t - 1) * row_bytes))
             nc.sync.dma_start(scale_rows[t][:], scale_dealt[:, t, :])
         w_codes = sb.tile([P, N], U32, name="w_codes", align_bytes=64)
         w_scales = sb.tile([P, N], U8, name="w_scales", align_bytes=64)
@@ -81,14 +83,14 @@ def tile_picked_none_po_kernel(
         for cols in (first, second):
             nc.vector.tensor_copy(x_picked[:, cols], x_table[:].bitcast(U32).indirect(entries(offs_sb, cols)))
 
-        EARLY = 384
-        early, late, third = slice(0, EARLY), slice(EARLY, S), quarters[2]
+        third, late = quarters[2], quarters[3]
+        EARLY = late.start
+        early, middle = slice(0, EARLY), slice(QUARTER, EARLY)
 
-        def product(t, cols):
-            acc = psum.tile([P, cols.stop - cols.start], F32, name=f"acc{t}_{cols.start}")
+        def product(dst, t, cols):
             wc = slice(t * P, (t + 1) * P)
             nc.tensor.matmul_mx(
-                out=acc[:],
+                out=dst,
                 lhsT=w_codes[:, wc].bitcast(FP8X4),
                 lhsT_scale=w_scales[:, wc],
                 rhs=x_picked[:, cols].bitcast(FP8X4),
@@ -96,46 +98,60 @@ def tile_picked_none_po_kernel(
                 start=True,
                 stop=True,
             )
-            return acc
 
-        prod1 = sb.tile([P, S], F32, name="prod1", align_bytes=64)
-        prod2 = sb.tile([P, S], F32, name="prod2", align_bytes=64)
-        prod3_head = sb.tile([P, QUARTER], F32, name="prod3_head", tag="shared", align_bytes=64)
-        prod3 = sb.tile([P, S], F32, name="prod3", align_bytes=64)
-        acc0_first = product(0, first)
-        nc.scalar.copy(prod1[:, first], product(1, first)[:])
-        acc0_second = product(0, second)
-        nc.scalar.copy(prod1[:, second], product(1, second)[:])
-        nc.scalar.copy(prod2[:], product(2, whole)[:])
-        acc3 = product(3, whole)
-        nc.scalar.copy(prod3_head[:], acc3[:, quarters[0]])
-        nc.scalar.copy(prod3[:, QUARTER:], acc3[:, QUARTER:])
+        y = sb.tile([P, PACK * S], F32, name="y", align_bytes=64)
+        y_early = y[:, : PACK * EARLY].rearrange("p (t c) -> p t c", t=PACK)
+        y_late = y[:, PACK * EARLY :].rearrange("p (t c) -> p t c", t=PACK)
+        y_quarters = y[:].rearrange("p (b c) -> p b c", c=QUARTER)
+        prod = sb.tile([P, 2, EARLY], F32, name="prod", align_bytes=64)
+        prod_late = sb.tile([P, PACK - 1, QUARTER], F32, name="prod_late", align_bytes=64)
+        acc0 = [psum.tile([P, HALF], F32, name=f"acc0_{h}") for h in range(2)]
+        acc = {t: psum.tile([P, EARLY], F32, name=f"acc{t}") for t in (1, 2, 3)}
+        acc_late = psum.tile([P, PACK - 1, QUARTER], F32, name="acc_late")
+
+        def early_product(t):
+            product(acc[t][:, first], t, first)
+            product(acc[t][:, third], t, third)
+
+        early_product(1)
+        nc.scalar.copy(prod[:, 0, :], acc[1][:])
+        product(acc0[0][:], 0, first)
+        product(acc0[1][:], 0, second)
+        early_product(2)
+        nc.scalar.copy(prod[:, 1, :], acc[2][:])
+        early_product(3)
+        head3, rest3 = y_late[:, 3, :], y[:, PACK * EARLY + QUARTER : PACK * EARLY + 3 * QUARTER]
+        nc.scalar.copy(head3, acc[3][:, quarters[0]])
+        nc.scalar.copy(rest3, acc[3][:, middle])
+        for t in (1, 2, 3):
+            product(acc_late[:, t - 1, :], t, late)
+        nc.scalar.copy(prod_late[:], acc_late[:])
 
         out_dealt = out_0.rearrange("(p t) s -> p t s", t=PACK)
-        y_early = sb.tile([P, PACK, EARLY], F32, name="y_early", align_bytes=64)
         picked0 = sb.tile([P, S], F32, name="picked0", align_bytes=64)
         for cols in (first, second):
             nc.vector.tensor_copy(picked0[:, cols], scale_rows[0][:].indirect(entries(task_sb, cols)))
-        nc.vector.tensor_tensor(y_early[:, 0, first], acc0_first[:], picked0[:, first], MULT)
-        nc.vector.tensor_tensor(y_early[:, 0, third], acc0_second[:, :QUARTER], picked0[:, third], MULT)
+        nc.vector.tensor_tensor(y_early[:, 0, first], acc0[0][:], picked0[:, first], MULT)
+        nc.vector.tensor_tensor(
+            y_quarters[:, 2:13:10, :],
+            acc0[1][:].rearrange("p (b c) -> p b c", c=QUARTER),
+            picked0[:, second].rearrange("p (b c) -> p b c", c=QUARTER),
+            MULT,
+        )
         nc.sync.dma_start(out_dealt[:, 0, early], y_early[:, 0, :])
 
         def scaled(dst, t, cols, src):
             nc.vector.tensor_tensor(dst, scale_rows[t][:].indirect(entries(task_sb, cols)), src, MULT)
 
-        for t, prod in ((1, prod1), (2, prod2)):
-            scaled(y_early[:, t, :], t, early, prod[:, early])
+        for t in (1, 2):
+            scaled(y_early[:, t, :], t, early, prod[:, t - 1, :])
             nc.sync.dma_start(out_dealt[:, t, early], y_early[:, t, :])
-        scaled(y_early[:, 3, quarters[0]], 3, quarters[0], prod3_head[:])
-        for cols in quarters[1:3]:
-            scaled(y_early[:, 3, cols], 3, cols, prod3[:, cols])
+        scaled(y_early[:, 3, quarters[0]], 3, quarters[0], head3)
+        scaled(y_early[:, 3, middle], 3, middle, rest3)
         nc.sync.dma_start(out_dealt[:, 3, early], y_early[:, 3, :])
-
-        y_late = sb.tile([P, PACK, S - EARLY], F32, name="y_late", tag="shared", align_bytes=64)
-        nc.vector.tensor_tensor(y_late[:, 0, :], acc0_second[:, QUARTER:], picked0[:, late], MULT)
-        for t, prod in ((1, prod1), (2, prod2), (3, prod3)):
-            scaled(y_late[:, t, :], t, late, prod[:, late])
-        nc.sync.dma_start(out_dealt[:, :, late], y_late[:])
+        for t in (1, 2, 3):
+            scaled(y_late[:, t, :], t, late, prod_late[:, t - 1, :])
+        nc.sync.dma_start(out_dealt[:, :, late], y_late)
 
         y_codes = sb.tile([P, S], I32, name="y_codes", align_bytes=64)
         y_scales = sb.tile([P, S], U8, name="y_scales", align_bytes=64)

@@ -34,38 +34,39 @@ def tile_picked_none_po_kernel(
         task_sb = lists.tile([P, S // PER_COL], U16, name="task_sb")
         turns = ctx.enter_context(tc.tile_pool(name="turns", bufs=1))
         row_bytes = 4 * U
-        w_raw = turns.tile([P, PACK, N], F32, name="w_raw", offset=row_bytes)
-        xs_table = turns.tile([P, T], U8, name="xs_table", offset=0)
+        w_raw = turns.tile([P, PACK, N], F32, name="w_raw", offset=2 * row_bytes)
+        xs_table = sb.tile([P, T], U8, name="xs_table", align_bytes=64)
         x_table = sb.tile([P, T], I32, name="x_table", align_bytes=64)
-        xs_picked = sb.tile([P, S], U8, name="xs_picked", align_bytes=64)
+        xs_picked = turns.tile([P, S], U8, name="xs_picked", offset=row_bytes - S // 2)
         xs_placed = sb.tile([P, S], U8, name="xs_placed", align_bytes=64)
 
         nc.vector.memset(xs_table[:].bitcast(I32), 0)
-        nc.vector.memset(xs_placed[:].bitcast(I32), 0)
         x_rows = x_words[0].rearrange("p c r -> p (c r)").bitcast(I32)
         w_dealt = w1.rearrange("(p j) m -> p j m", j=PACK)
-        nc.sync.dma_start(w_raw[:, :, : N // 2], w_dealt[:, :, : N // 2])
+        nc.sync.dma_start(w_raw[:, :, :128], w_dealt[:, :, :128])
         nc.sync.dma_start(offs_sb[:], offs)
-        nc.sync.dma_start(xs_table[0:P:8, :].bitcast(I32), x_scales[0].bitcast(I32))
-        nc.sync.dma_start(w_raw[:, :, N // 2 :], w_dealt[:, :, N // 2 :])
-        nc.sync.dma_start(x_table[:], x_rows)
         nc.sync.dma_start(task_sb[:], task)
+        nc.sync.dma_start(xs_table[0:P:8, :].bitcast(I32), x_scales[0].bitcast(I32))
+        nc.sync.dma_start(w_raw[:, :, 128:], w_dealt[:, :, 128:])
+        nc.sync.dma_start(x_table[:], x_rows)
         scale_dealt = scale.rearrange("(p t) u -> p t u", t=PACK)
-        scale_rows = [sb.tile([P, U], F32, name="scale_rows0", align_bytes=64)]
-        nc.sync.dma_start(scale_rows[0][:], scale_dealt[:, 0, :])
+        scale_rows = []
 
         nc.vector.tensor_copy(xs_picked[:], xs_table[:].indirect(offs_sb[:]))
-        for r in range(4):
-            nc.sync.dma_start(xs_placed[r:P:32, :].bitcast(I32), xs_picked[8 * r : P : 32, :].bitcast(I32))
+        nc.vector.tensor_copy(xs_placed[:].bitcast(I32), xs_picked[:].bitcast(I32))
+        for r in range(1, 4):
+            nc.sync.dma_start(xs_placed[r:P:32, :].bitcast(I32), xs_placed[8 * r : P : 32, :].bitcast(I32))
 
         w_bf = sb.tile([P, PACK, P, PACK], BF16, name="w_bf", align_bytes=64)
-        w_src = w_raw[:].rearrange("p j (m t) -> p m t j", t=PACK)
-        w_dst = w_bf[:].rearrange("p t m j -> p m t j")
-        nc.scalar.copy(w_dst[:, 0:64], w_src[:, 0:64])
-        nc.vector.tensor_copy(w_dst[:, 64:104], w_src[:, 64:104])
-        nc.scalar.copy(w_dst[:, 104:P], w_src[:, 104:P])
-        for t in range(1, PACK):
-            scale_rows.append(turns.tile([P, U], F32, name=f"scale_rows{t}", offset=(t - 1) * row_bytes))
+        w_src = w_raw[:].rearrange("p j (m u e) -> p u m j e", u=2, e=2)
+        w_dst = w_bf[:].rearrange("p (u e) m j -> p u m j e", u=2)
+        nc.scalar.copy(
+            w_bf[:].rearrange("p t m j -> p m t j")[:, 0:32], w_raw[:].rearrange("p j (m t) -> p m t j", t=PACK)[:, 0:32]
+        )
+        nc.vector.tensor_copy(w_dst[:, :, 32:88], w_src[:, :, 32:88])
+        nc.scalar.copy(w_dst[:, :, 88:P], w_src[:, :, 88:P])
+        for t in range(PACK):
+            scale_rows.append(turns.tile([P, U], F32, name=f"scale_rows{t}", offset=t * row_bytes))
             nc.sync.dma_start(scale_rows[t][:], scale_dealt[:, t, :])
         w_codes = sb.tile([P, N], U32, name="w_codes", align_bytes=64)
         w_scales = sb.tile([P, N], U8, name="w_scales", align_bytes=64)
@@ -113,9 +114,10 @@ def tile_picked_none_po_kernel(
             product(acc[t][:, first], t, first)
             product(acc[t][:, third], t, third)
 
-        early_product(1)
-        nc.scalar.copy(prod[:, 0, :], acc[1][:])
+        product(acc[1][:, first], 1, first)
         product(acc0[0][:], 0, first)
+        product(acc[1][:, third], 1, third)
+        nc.scalar.copy(prod[:, 0, :], acc[1][:])
         product(acc0[1][:], 0, second)
         early_product(2)
         nc.scalar.copy(prod[:, 1, :], acc[2][:])
@@ -159,7 +161,7 @@ def tile_picked_none_po_kernel(
         y_bf = sb.tile([P, S, PACK], BF16, name="y_bf", align_bytes=64)
 
         def rounded(copy, cols, src):
-            copy(y_bf[:, cols].rearrange("p (c i) t -> p c t i", i=4), src.rearrange("p t (c i) -> p c t i", i=4))
+            copy(y_bf[:, cols].rearrange("p (c i) t -> p c t i", i=2), src.rearrange("p t (c i) -> p c t i", i=2))
 
         def quantised(cols):
             nc.vector.quantize_mx(

@@ -43,11 +43,11 @@ def tile_picked_none_po_kernel(
         nc.vector.memset(xs_table[:].bitcast(I32), 0)
         x_rows = x_words[0].rearrange("p c r -> p (c r)").bitcast(I32)
         w_dealt = w1.rearrange("(p j) m -> p j m", j=PACK)
-        nc.sync.dma_start(w_raw[:, :, :128], w_dealt[:, :, :128])
+        nc.sync.dma_start(w_raw[:, :1], w_dealt[:, :1])
         nc.sync.dma_start(offs_sb[:], offs)
         nc.sync.dma_start(task_sb[:], task)
         nc.sync.dma_start(xs_table[0:P:8, :].bitcast(I32), x_scales[0].bitcast(I32))
-        nc.sync.dma_start(w_raw[:, :, 128:], w_dealt[:, :, 128:])
+        nc.sync.dma_start(w_raw[:, 1:], w_dealt[:, 1:])
         nc.sync.dma_start(x_table[:], x_rows)
         scale_dealt = scale.rearrange("(p t) u -> p t u", t=PACK)
         scale_rows = []
@@ -60,19 +60,19 @@ def tile_picked_none_po_kernel(
         w_bf = sb.tile([P, PACK, P, PACK], BF16, name="w_bf", align_bytes=64)
         w_src = w_raw[:].rearrange("p j (m u e) -> p u m j e", u=2, e=2)
         w_dst = w_bf[:].rearrange("p (u e) m j -> p u m j e", u=2)
-        nc.scalar.copy(
-            w_bf[:].rearrange("p t m j -> p m t j")[:, 0:32], w_raw[:].rearrange("p j (m t) -> p m t j", t=PACK)[:, 0:32]
-        )
-        nc.vector.tensor_copy(w_dst[:, :, 32:88], w_src[:, :, 32:88])
-        nc.scalar.copy(w_dst[:, :, 88:P], w_src[:, :, 88:P])
+        for u in range(2):
+            nc.vector.tensor_copy(w_dst[:, u], w_src[:, u])
         for t in range(PACK):
             scale_rows.append(turns.tile([P, U], F32, name=f"scale_rows{t}", offset=t * row_bytes))
             nc.sync.dma_start(scale_rows[t][:], scale_dealt[:, t, :])
         w_codes = sb.tile([P, N], U32, name="w_codes", align_bytes=64)
         w_scales = sb.tile([P, N], U8, name="w_scales", align_bytes=64)
-        nc.vector.quantize_mx(
-            out=w_codes[:].bitcast(FP8X4), scales=w_scales[:], in_=w_bf[:].rearrange("p t m j -> p (t m j)")
-        )
+        for u in range(2):
+            nc.vector.quantize_mx(
+                out=w_codes[:, 2 * u * P : 2 * (u + 1) * P].bitcast(FP8X4),
+                scales=w_scales[:, 2 * u * P : 2 * (u + 1) * P],
+                in_=w_bf[:, 2 * u : 2 * u + 2].rearrange("p t m j -> p (t m j)"),
+            )
 
         def entries(lst, cols):
             return lst[:, cols.start // PER_COL : cols.stop // PER_COL]

@@ -19,6 +19,8 @@ PACK = 4
 HALF = S // 2
 QUARTER = S // 4
 PER_COL = 16
+HEAD = 64
+SHARE = 64
 
 
 def tile_picked_none_po_kernel(
@@ -78,7 +80,7 @@ def tile_picked_none_po_kernel(
             return lst[:, cols.start // PER_COL : cols.stop // PER_COL]
 
         quarters = [slice(q * QUARTER, (q + 1) * QUARTER) for q in range(4)]
-        first, second, whole = slice(0, HALF), slice(HALF, S), slice(0, S)
+        first, second = slice(0, HALF), slice(HALF, S)
 
         x_picked = sb.tile([P, S], U32, name="x_picked", align_bytes=64)
         for cols in (first, second):
@@ -86,9 +88,9 @@ def tile_picked_none_po_kernel(
 
         third, late = quarters[2], quarters[3]
         EARLY = late.start
-        early, middle = slice(0, EARLY), slice(QUARTER, EARLY)
+        early = slice(0, EARLY)
 
-        def product(dst, t, cols):
+        def matmul(dst, t, cols):
             wc = slice(t * P, (t + 1) * P)
             nc.tensor.matmul_mx(
                 out=dst,
@@ -104,56 +106,56 @@ def tile_picked_none_po_kernel(
         y_early = y[:, : PACK * EARLY].rearrange("p (t c) -> p t c", t=PACK)
         y_late = y[:, PACK * EARLY :].rearrange("p (t c) -> p t c", t=PACK)
         y_quarters = y[:].rearrange("p (b c) -> p b c", c=QUARTER)
-        prod = sb.tile([P, 2, EARLY], F32, name="prod", align_bytes=64)
-        prod_late = sb.tile([P, PACK - 1, QUARTER], F32, name="prod_late", align_bytes=64)
-        acc0 = [psum.tile([P, HALF], F32, name=f"acc0_{h}") for h in range(2)]
-        acc = {t: psum.tile([P, EARLY], F32, name=f"acc{t}") for t in (1, 2, 3)}
+        prod = sb.tile([P, PACK, S], F32, name="prod", align_bytes=64)
+
+        def product(t, *pieces):
+            start = pieces[0].start
+            acc = psum.tile([P, pieces[-1].stop - start], F32, name=f"acc{t}_{start}")
+            for cols in pieces:
+                matmul(acc[:, cols.start - start : cols.stop - start], t, cols)
+            return acc
+
+        nc.scalar.copy(prod[:, 0, first], product(0, first)[:])
+        parked1 = y[:, PACK * EARLY - QUARTER : PACK * EARLY + QUARTER]
+        nc.scalar.copy(parked1, product(1, first)[:])
+        nc.scalar.copy(prod[:, 1, third], product(1, third)[:])
+        nc.scalar.copy(prod[:, 2, early], product(2, first, third)[:])
+        acc0 = product(0, second)
+        acc3 = product(3, first, third)
+        parked3 = y[:, PACK * EARLY + HALF - HEAD // 2 : PACK * EARLY + HALF + HEAD // 2]
+        nc.scalar.copy(parked3, acc3[:, :HEAD])
+        nc.scalar.copy(prod[:, 3, HEAD:EARLY], acc3[:, HEAD:])
         acc_late = psum.tile([P, PACK - 1, QUARTER], F32, name="acc_late")
-
-        def early_product(t):
-            product(acc[t][:, first], t, first)
-            product(acc[t][:, third], t, third)
-
-        product(acc[1][:, first], 1, first)
-        product(acc0[0][:], 0, first)
-        product(acc[1][:, third], 1, third)
-        nc.scalar.copy(prod[:, 0, :], acc[1][:])
-        product(acc0[1][:], 0, second)
-        early_product(2)
-        nc.scalar.copy(prod[:, 1, :], acc[2][:])
-        early_product(3)
-        head3, rest3 = y_late[:, 3, :], y[:, PACK * EARLY + QUARTER : PACK * EARLY + 3 * QUARTER]
-        nc.scalar.copy(head3, acc[3][:, quarters[0]])
-        nc.scalar.copy(rest3, acc[3][:, middle])
         for t in (1, 2, 3):
-            product(acc_late[:, t - 1, :], t, late)
-        nc.scalar.copy(prod_late[:], acc_late[:])
-
-        out_dealt = out_0.rearrange("(p t) s -> p t s", t=PACK)
-        picked0 = sb.tile([P, S], F32, name="picked0", align_bytes=64)
-        for cols in (first, second):
-            nc.vector.tensor_copy(picked0[:, cols], scale_rows[0][:].indirect(entries(task_sb, cols)))
-        nc.vector.tensor_tensor(y_early[:, 0, first], acc0[0][:], picked0[:, first], MULT)
-        nc.vector.tensor_tensor(
-            y_quarters[:, 2:13:10, :],
-            acc0[1][:].rearrange("p (b c) -> p b c", c=QUARTER),
-            picked0[:, second].rearrange("p (b c) -> p b c", c=QUARTER),
-            MULT,
-        )
-        nc.sync.dma_start(out_dealt[:, 0, early], y_early[:, 0, :])
+            matmul(acc_late[:, t - 1, :], t, late)
+        nc.scalar.copy(prod[:, 1:, late], acc_late[:])
 
         def scaled(dst, t, cols, src):
             nc.vector.tensor_tensor(dst, scale_rows[t][:].indirect(entries(task_sb, cols)), src, MULT)
 
-        for t in (1, 2):
-            scaled(y_early[:, t, :], t, early, prod[:, t - 1, :])
-            nc.sync.dma_start(out_dealt[:, t, early], y_early[:, t, :])
-        scaled(y_early[:, 3, quarters[0]], 3, quarters[0], head3)
-        scaled(y_early[:, 3, middle], 3, middle, rest3)
+        out_dealt = out_0.rearrange("(p t) s -> p t s", t=PACK)
+        picked0 = prod[:, 0, second]
+        nc.vector.tensor_copy(picked0, scale_rows[0][:].indirect(entries(task_sb, second)))
+        scaled(y_early[:, 0, first], 0, first, prod[:, 0, first])
+        scaled(y_early[:, 1, first], 1, first, parked1)
+        scaled(y_early[:, 1, third], 1, third, prod[:, 1, third])
+        nc.vector.tensor_tensor(
+            y_quarters[:, 2:13:10, :],
+            acc0[:].rearrange("p (b c) -> p b c", c=QUARTER),
+            picked0.rearrange("p (b c) -> p b c", c=QUARTER),
+            MULT,
+        )
+        nc.sync.dma_start(out_dealt[:, :2, early], y_early[:, :2, :])
+        nc.sync.dma_start(out_dealt[:, 0, late], y_late[:, 0, :])
+        scaled(y_early[:, 2, :], 2, early, prod[:, 2, early])
+        nc.sync.dma_start(out_dealt[:, 2, early], y_early[:, 2, :])
+        scaled(y_early[:, 3, :HEAD], 3, slice(0, HEAD), parked3)
+        for cols in (slice(HEAD, 192), slice(192, EARLY)):
+            scaled(y_early[:, 3, cols], 3, cols, prod[:, 3, cols])
         nc.sync.dma_start(out_dealt[:, 3, early], y_early[:, 3, :])
         for t in (1, 2, 3):
-            scaled(y_late[:, t, :], t, late, prod_late[:, t - 1, :])
-        nc.sync.dma_start(out_dealt[:, :, late], y_late)
+            scaled(y_late[:, t, :], t, late, prod[:, t, late])
+        nc.sync.dma_start(out_dealt[:, 1:, late], y_late[:, 1:, :])
 
         y_codes = sb.tile([P, S], I32, name="y_codes", align_bytes=64)
         y_scales = sb.tile([P, S], U8, name="y_scales", align_bytes=64)
@@ -170,12 +172,12 @@ def tile_picked_none_po_kernel(
                 in_=y_bf[:, cols].rearrange("p c t -> p (c t)"),
             )
 
-        for cols in quarters[:3]:
+        for cols in (slice(0, HEAD), slice(HEAD, 192), slice(192, HALF), third):
             rounded(nc.scalar.copy, cols, y_early[:, :, cols])
-        rounded(nc.scalar.copy, slice(EARLY, EARLY + 64), y_late[:, :, 0:64])
+        rounded(nc.scalar.copy, slice(EARLY, EARLY + SHARE), y_late[:, :, :SHARE])
         quantised(first)
         nc.sync.dma_start(words_out[:, first], y_codes[:, first])
-        rounded(nc.vector.tensor_copy, slice(EARLY + 64, S), y_late[:, :, 64:128])
+        rounded(nc.vector.tensor_copy, slice(EARLY + SHARE, S), y_late[:, :, SHARE:])
         quantised(third)
         quantised(late)
         nc.sync.dma_start(words_out[:, second], y_codes[:, second])

@@ -20,7 +20,7 @@ HALF = S // 2
 QUARTER = S // 4
 PER_COL = 16
 HEAD = 64
-SHARE = 64
+SHARE = 32
 
 
 def tile_picked_none_po_kernel(
@@ -118,17 +118,17 @@ def tile_picked_none_po_kernel(
         nc.scalar.copy(prod[:, 0, first], product(0, first)[:])
         parked1 = y[:, PACK * EARLY - QUARTER : PACK * EARLY + QUARTER]
         nc.scalar.copy(parked1, product(1, first)[:])
-        nc.scalar.copy(prod[:, 1, third], product(1, third)[:])
+        nc.scalar.copy(prod[:, 1, second], product(1, second)[:])
         nc.scalar.copy(prod[:, 2, early], product(2, first, third)[:])
         acc0 = product(0, second)
         acc3 = product(3, first, third)
-        parked3 = y[:, PACK * EARLY + HALF - HEAD // 2 : PACK * EARLY + HALF + HEAD // 2]
+        parked3 = y_late[:, 2, :HEAD]
         nc.scalar.copy(parked3, acc3[:, :HEAD])
         nc.scalar.copy(prod[:, 3, HEAD:EARLY], acc3[:, HEAD:])
-        acc_late = psum.tile([P, PACK - 1, QUARTER], F32, name="acc_late")
-        for t in (1, 2, 3):
-            matmul(acc_late[:, t - 1, :], t, late)
-        nc.scalar.copy(prod[:, 1:, late], acc_late[:])
+        acc_late = psum.tile([P, 2, QUARTER], F32, name="acc_late")
+        for t in (2, 3):
+            matmul(acc_late[:, t - 2, :], t, late)
+        nc.scalar.copy(prod[:, 2:, late], acc_late[:])
 
         def scaled(dst, t, cols, src):
             nc.vector.tensor_tensor(dst, scale_rows[t][:].indirect(entries(task_sb, cols)), src, MULT)
@@ -139,6 +139,7 @@ def tile_picked_none_po_kernel(
         scaled(y_early[:, 0, first], 0, first, prod[:, 0, first])
         scaled(y_early[:, 1, first], 1, first, parked1)
         scaled(y_early[:, 1, third], 1, third, prod[:, 1, third])
+        scaled(y_late[:, 1, :], 1, late, prod[:, 1, late])
         nc.vector.tensor_tensor(
             y_quarters[:, 2:13:10, :],
             acc0[:].rearrange("p (b c) -> p b c", c=QUARTER),
@@ -146,16 +147,16 @@ def tile_picked_none_po_kernel(
             MULT,
         )
         nc.sync.dma_start(out_dealt[:, :2, early], y_early[:, :2, :])
-        nc.sync.dma_start(out_dealt[:, 0, late], y_late[:, 0, :])
+        nc.sync.dma_start(out_dealt[:, :2, late], y_late[:, :2, :])
         scaled(y_early[:, 2, :], 2, early, prod[:, 2, early])
         nc.sync.dma_start(out_dealt[:, 2, early], y_early[:, 2, :])
         scaled(y_early[:, 3, :HEAD], 3, slice(0, HEAD), parked3)
         for cols in (slice(HEAD, 192), slice(192, EARLY)):
             scaled(y_early[:, 3, cols], 3, cols, prod[:, 3, cols])
         nc.sync.dma_start(out_dealt[:, 3, early], y_early[:, 3, :])
-        for t in (1, 2, 3):
+        for t in (2, 3):
             scaled(y_late[:, t, :], t, late, prod[:, t, late])
-        nc.sync.dma_start(out_dealt[:, 1:, late], y_late[:, 1:, :])
+        nc.sync.dma_start(out_dealt[:, 2:, late], y_late[:, 2:, :])
 
         y_codes = sb.tile([P, S], I32, name="y_codes", align_bytes=64)
         y_scales = sb.tile([P, S], U8, name="y_scales", align_bytes=64)

@@ -20,7 +20,7 @@ HALF = S // 2
 QUARTER = S // 4
 PER_COL = 16
 HEAD = 64
-SHARE = 32
+SHARE = 64
 
 
 def tile_picked_none_po_kernel(
@@ -37,27 +37,28 @@ def tile_picked_none_po_kernel(
         turns = ctx.enter_context(tc.tile_pool(name="turns", bufs=1))
         row_bytes = 4 * U
         w_raw = turns.tile([P, PACK, N], F32, name="w_raw", offset=2 * row_bytes)
-        xs_table = sb.tile([P, T], U8, name="xs_table", align_bytes=64)
+        xs_table = turns.tile([P, T], U8, name="xs_table", offset=row_bytes - T // 2)
         x_table = sb.tile([P, T], I32, name="x_table", align_bytes=64)
-        xs_picked = turns.tile([P, S], U8, name="xs_picked", offset=row_bytes - S // 2)
+        xs_picked = sb.tile([P, S], U8, name="xs_picked", align_bytes=64)
         xs_placed = sb.tile([P, S], U8, name="xs_placed", align_bytes=64)
 
         nc.vector.memset(xs_table[:].bitcast(I32), 0)
+        nc.vector.memset(xs_placed[:].bitcast(I32), 0)
         x_rows = x_words[0].rearrange("p c r -> p (c r)").bitcast(I32)
         w_dealt = w1.rearrange("(p j) m -> p j m", j=PACK)
         nc.sync.dma_start(w_raw[:, :1], w_dealt[:, :1])
         nc.sync.dma_start(offs_sb[:], offs)
         nc.sync.dma_start(task_sb[:], task)
-        nc.sync.dma_start(xs_table[0:P:8, :].bitcast(I32), x_scales[0].bitcast(I32))
+        nc.sync.dma_start(xs_table[0:16, :].bitcast(I32), x_scales[0].bitcast(I32))
         nc.sync.dma_start(w_raw[:, 1:], w_dealt[:, 1:])
         nc.sync.dma_start(x_table[:], x_rows)
         scale_dealt = scale.rearrange("(p t) u -> p t u", t=PACK)
         scale_rows = []
 
         nc.vector.tensor_copy(xs_picked[:], xs_table[:].indirect(offs_sb[:]))
-        nc.vector.tensor_copy(xs_placed[:].bitcast(I32), xs_picked[:].bitcast(I32))
-        for r in range(1, 4):
-            nc.sync.dma_start(xs_placed[r:P:32, :].bitcast(I32), xs_placed[8 * r : P : 32, :].bitcast(I32))
+        for q in range(1, 4):
+            nc.sync.dma_start(xs_placed[32 * q : 32 * q + 4, :].bitcast(I32), xs_picked[4 * q : 4 * q + 4, :].bitcast(I32))
+        nc.vector.tensor_copy(xs_placed[:32, :].bitcast(I32), xs_picked[:32, :].bitcast(I32))
 
         w_bf = sb.tile([P, PACK, P, PACK], BF16, name="w_bf", align_bytes=64)
         w_src = w_raw[:].rearrange("p j (m u e) -> p u m j e", u=2, e=2)
@@ -102,10 +103,9 @@ def tile_picked_none_po_kernel(
                 stop=True,
             )
 
-        y = sb.tile([P, PACK * S], F32, name="y", align_bytes=64)
-        y_early = y[:, : PACK * EARLY].rearrange("p (t c) -> p t c", t=PACK)
-        y_late = y[:, PACK * EARLY :].rearrange("p (t c) -> p t c", t=PACK)
-        y_quarters = y[:].rearrange("p (b c) -> p b c", c=QUARTER)
+        y = sb.tile([P, PACK * (PACK - 1) * S], F32, name="y", align_bytes=64)
+        y_early = y[:, : PACK * S].rearrange("p (t c) -> p t c", t=PACK)[:, :, early]
+        y_late = y[:].rearrange("p (t c) -> p t c", t=PACK)[:, :, late]
         prod = sb.tile([P, PACK, S], F32, name="prod", align_bytes=64)
 
         def product(t, *pieces):
@@ -115,12 +115,12 @@ def tile_picked_none_po_kernel(
                 matmul(acc[:, cols.start - start : cols.stop - start], t, cols)
             return acc
 
-        nc.scalar.copy(prod[:, 0, first], product(0, first)[:])
-        parked1 = y[:, PACK * EARLY - QUARTER : PACK * EARLY + QUARTER]
+        nc.scalar.copy(prod[:, 0, quarters[0]], product(0, quarters[0])[:])
+        parked1 = y[:, second]
         nc.scalar.copy(parked1, product(1, first)[:])
         nc.scalar.copy(prod[:, 1, second], product(1, second)[:])
         nc.scalar.copy(prod[:, 2, early], product(2, first, third)[:])
-        acc0 = product(0, second)
+        acc0 = product(0, quarters[1], second)
         acc3 = product(3, first, third)
         parked3 = y_late[:, 2, :HEAD]
         nc.scalar.copy(parked3, acc3[:, :HEAD])
@@ -134,20 +134,16 @@ def tile_picked_none_po_kernel(
             nc.vector.tensor_tensor(dst, scale_rows[t][:].indirect(entries(task_sb, cols)), src, MULT)
 
         out_dealt = out_0.rearrange("(p t) s -> p t s", t=PACK)
-        picked0 = prod[:, 0, second]
-        nc.vector.tensor_copy(picked0, scale_rows[0][:].indirect(entries(task_sb, second)))
-        scaled(y_early[:, 0, first], 0, first, prod[:, 0, first])
+        rest = slice(QUARTER, S)
+        picked0 = prod[:, 0, rest]
+        nc.vector.tensor_copy(picked0, scale_rows[0][:].indirect(entries(task_sb, rest)))
+        scaled(y_early[:, 0, quarters[0]], 0, quarters[0], prod[:, 0, quarters[0]])
         scaled(y_early[:, 1, first], 1, first, parked1)
         scaled(y_early[:, 1, third], 1, third, prod[:, 1, third])
         scaled(y_late[:, 1, :], 1, late, prod[:, 1, late])
-        nc.vector.tensor_tensor(
-            y_quarters[:, 2:13:10, :],
-            acc0[:].rearrange("p (b c) -> p b c", c=QUARTER),
-            picked0.rearrange("p (b c) -> p b c", c=QUARTER),
-            MULT,
-        )
-        nc.sync.dma_start(out_dealt[:, :2, early], y_early[:, :2, :])
-        nc.sync.dma_start(out_dealt[:, :2, late], y_late[:, :2, :])
+        nc.sync.dma_start(out_dealt[:, 1, late], y_late[:, 1, :])
+        nc.vector.tensor_tensor(y[:, rest], acc0[:], picked0, MULT)
+        nc.sync.dma_start(out_0.rearrange("(p t) s -> p (t s)", t=PACK)[:, : S + EARLY], y[:, : S + EARLY])
         scaled(y_early[:, 2, :], 2, early, prod[:, 2, early])
         nc.sync.dma_start(out_dealt[:, 2, early], y_early[:, 2, :])
         scaled(y_early[:, 3, :HEAD], 3, slice(0, HEAD), parked3)
@@ -164,7 +160,7 @@ def tile_picked_none_po_kernel(
         y_bf = sb.tile([P, S, PACK], BF16, name="y_bf", align_bytes=64)
 
         def rounded(copy, cols, src):
-            copy(y_bf[:, cols].rearrange("p (c i) t -> p c t i", i=2), src.rearrange("p t (c i) -> p c t i", i=2))
+            copy(y_bf[:, cols].rearrange("p (c i) t -> p c t i", i=4), src.rearrange("p t (c i) -> p c t i", i=4))
 
         def quantised(cols):
             nc.vector.quantize_mx(
@@ -173,12 +169,13 @@ def tile_picked_none_po_kernel(
                 in_=y_bf[:, cols].rearrange("p c t -> p (c t)"),
             )
 
-        for cols in (slice(0, HEAD), slice(HEAD, 192), slice(192, HALF), third):
+        for cols in (slice(0, HEAD), slice(HEAD, 192), slice(192, HALF), slice(HALF, HALF + SHARE)):
             rounded(nc.scalar.copy, cols, y_early[:, :, cols])
         rounded(nc.scalar.copy, slice(EARLY, EARLY + SHARE), y_late[:, :, :SHARE])
+        rounded(nc.vector.tensor_copy, slice(HALF + SHARE, EARLY), y_early[:, :, HALF + SHARE :])
+        rounded(nc.vector.tensor_copy, slice(EARLY + SHARE, S), y_late[:, :, SHARE:])
         quantised(first)
         nc.sync.dma_start(words_out[:, first], y_codes[:, first])
-        rounded(nc.vector.tensor_copy, slice(EARLY + SHARE, S), y_late[:, :, SHARE:])
         quantised(third)
         quantised(late)
         nc.sync.dma_start(words_out[:, second], y_codes[:, second])

@@ -36,26 +36,27 @@ def tile_picked_none_po_kernel(
         task_sb = lists.tile([P, S // PER_COL], U16, name="task_sb")
         turns = ctx.enter_context(tc.tile_pool(name="turns", bufs=1))
         row_bytes = 4 * U
-        w_raw = turns.tile([P, PACK, N], F32, name="w_raw", offset=2 * row_bytes)
-        xs_table = turns.tile([P, T], U8, name="xs_table", offset=row_bytes - T // 2)
+        w_raw = sb.tile([P, PACK, N], F32, name="w_raw")
+        xs_room = turns.tile([P, 2 * row_bytes + 64], U8, name="xs_room", offset=row_bytes - 32)
+        xs_table = xs_room[:, :T]
         x_table = sb.tile([P, T], I32, name="x_table", align_bytes=64)
         xs_picked = sb.tile([P, S], U8, name="xs_picked", align_bytes=64)
         xs_placed = sb.tile([P, S], U8, name="xs_placed", align_bytes=64)
 
-        nc.vector.memset(xs_table[:].bitcast(I32), 0)
+        nc.vector.memset(xs_table.bitcast(I32), 0)
         nc.vector.memset(xs_placed[:].bitcast(I32), 0)
         x_rows = x_words[0].rearrange("p c r -> p (c r)").bitcast(I32)
         w_dealt = w1.rearrange("(p j) m -> p j m", j=PACK)
         nc.sync.dma_start(w_raw[:, :1], w_dealt[:, :1])
         nc.sync.dma_start(offs_sb[:], offs)
         nc.sync.dma_start(task_sb[:], task)
-        nc.sync.dma_start(xs_table[0:16, :].bitcast(I32), x_scales[0].bitcast(I32))
+        nc.sync.dma_start(xs_room[0:16, :T].bitcast(I32), x_scales[0].bitcast(I32))
         nc.sync.dma_start(w_raw[:, 1:], w_dealt[:, 1:])
         nc.sync.dma_start(x_table[:], x_rows)
         scale_dealt = scale.rearrange("(p t) u -> p t u", t=PACK)
         scale_rows = []
 
-        nc.vector.tensor_copy(xs_picked[:], xs_table[:].indirect(offs_sb[:]))
+        nc.vector.tensor_copy(xs_picked[:], xs_table.indirect(offs_sb[:]))
         for q in range(1, 4):
             nc.sync.dma_start(xs_placed[32 * q : 32 * q + 4, :].bitcast(I32), xs_picked[4 * q : 4 * q + 4, :].bitcast(I32))
         nc.vector.tensor_copy(xs_placed[:32, :].bitcast(I32), xs_picked[:32, :].bitcast(I32))

@@ -21,6 +21,7 @@ QUARTER = S // 4
 PER_COL = 16
 HEAD = 64
 SHARE = 64
+THIRD_SHARE = 32
 
 
 def tile_picked_none_po_kernel(
@@ -116,12 +117,13 @@ def tile_picked_none_po_kernel(
                 matmul(acc[:, cols.start - start : cols.stop - start], t, cols)
             return acc
 
-        nc.scalar.copy(prod[:, 0, quarters[0]], product(0, quarters[0])[:])
+        for cols in quarters[:2]:
+            nc.scalar.copy(prod[:, 0, cols], product(0, cols)[:])
         parked1 = y[:, second]
         nc.scalar.copy(parked1, product(1, first)[:])
         nc.scalar.copy(prod[:, 1, second], product(1, second)[:])
         nc.scalar.copy(prod[:, 2, early], product(2, first, third)[:])
-        acc0 = product(0, quarters[1], second)
+        acc0 = product(0, second)
         acc3 = product(3, first, third)
         parked3 = y_late[:, 2, :HEAD]
         nc.scalar.copy(parked3, acc3[:, :HEAD])
@@ -135,10 +137,11 @@ def tile_picked_none_po_kernel(
             nc.vector.tensor_tensor(dst, scale_rows[t][:].indirect(entries(task_sb, cols)), src, MULT)
 
         out_dealt = out_0.rearrange("(p t) s -> p t s", t=PACK)
-        rest = slice(QUARTER, S)
+        rest = second
         picked0 = prod[:, 0, rest]
         nc.vector.tensor_copy(picked0, scale_rows[0][:].indirect(entries(task_sb, rest)))
-        scaled(y_early[:, 0, quarters[0]], 0, quarters[0], prod[:, 0, quarters[0]])
+        for cols in quarters[:2]:
+            scaled(y_early[:, 0, cols], 0, cols, prod[:, 0, cols])
         scaled(y_early[:, 1, first], 1, first, parked1)
         scaled(y_early[:, 1, third], 1, third, prod[:, 1, third])
         scaled(y_late[:, 1, :], 1, late, prod[:, 1, late])
@@ -170,10 +173,10 @@ def tile_picked_none_po_kernel(
                 in_=y_bf[:, cols].rearrange("p c t -> p (c t)"),
             )
 
-        for cols in (slice(0, HEAD), slice(HEAD, 192), slice(192, HALF), slice(HALF, HALF + SHARE)):
+        for cols in (slice(0, HEAD), slice(HEAD, 192), slice(192, HALF), slice(HALF, HALF + THIRD_SHARE)):
             rounded(nc.scalar.copy, cols, y_early[:, :, cols])
         rounded(nc.scalar.copy, slice(EARLY, EARLY + SHARE), y_late[:, :, :SHARE])
-        rounded(nc.vector.tensor_copy, slice(HALF + SHARE, EARLY), y_early[:, :, HALF + SHARE :])
+        rounded(nc.vector.tensor_copy, slice(HALF + THIRD_SHARE, EARLY), y_early[:, :, HALF + THIRD_SHARE :])
         rounded(nc.vector.tensor_copy, slice(EARLY + SHARE, S), y_late[:, :, SHARE:])
         quantised(first)
         nc.sync.dma_start(words_out[:, first], y_codes[:, first])

@@ -13,15 +13,13 @@ U16 = mybir.dt.uint16
 U8 = mybir.dt.uint8
 FP8X4 = mybir.dt.float8_e4m3fn_x4
 MULT = mybir.AluOpType.mult
+COPY = mybir.ActivationFunctionType.Copy
 
 P = 128
 PACK = 4
 HALF = S // 2
 QUARTER = S // 4
 PER_COL = 16
-HEAD = 64
-SHARE = 64
-THIRD_SHARE = 32
 
 
 def tile_picked_none_po_kernel(
@@ -89,9 +87,6 @@ def tile_picked_none_po_kernel(
         for cols in (first, second):
             nc.vector.tensor_copy(x_picked[:, cols], x_table[:].bitcast(U32).indirect(entries(offs_sb, cols)))
 
-        third, late = quarters[2], quarters[3]
-        EARLY = late.start
-        early = slice(0, EARLY)
 
         def matmul(dst, t, cols):
             wc = slice(t * P, (t + 1) * P)
@@ -105,66 +100,66 @@ def tile_picked_none_po_kernel(
                 stop=True,
             )
 
-        y = sb.tile([P, PACK * (PACK - 1) * S], F32, name="y", align_bytes=64)
-        y_early = y[:, : PACK * S].rearrange("p (t c) -> p t c", t=PACK)[:, :, early]
-        y_late = y[:].rearrange("p (t c) -> p t c", t=PACK)[:, :, late]
-        prod = sb.tile([P, PACK, S], F32, name="prod", align_bytes=64)
-
-        def product(t, *pieces):
-            start = pieces[0].start
-            acc = psum.tile([P, pieces[-1].stop - start], F32, name=f"acc{t}_{start}")
-            for cols in pieces:
-                matmul(acc[:, cols.start - start : cols.stop - start], t, cols)
+        def product(t, cols):
+            acc = psum.tile([P, cols.stop - cols.start], F32, name=f"acc{t}_{cols.start}")
+            matmul(acc[:], t, cols)
             return acc
 
-        for cols in quarters[:2]:
-            nc.scalar.copy(prod[:, 0, cols], product(0, cols)[:])
-        parked1 = y[:, second]
-        nc.scalar.copy(parked1, product(1, first)[:])
-        nc.scalar.copy(prod[:, 1, second], product(1, second)[:])
-        nc.scalar.copy(prod[:, 2, early], product(2, first, third)[:])
-        acc0 = product(0, second)
-        acc3 = product(3, first, third)
-        parked3 = y_late[:, 2, :HEAD]
-        nc.scalar.copy(parked3, acc3[:, :HEAD])
-        nc.scalar.copy(prod[:, 3, HEAD:EARLY], acc3[:, HEAD:])
-        acc_late = psum.tile([P, 2, QUARTER], F32, name="acc_late")
-        for t in (2, 3):
-            matmul(acc_late[:, t - 2, :], t, late)
-        nc.scalar.copy(prod[:, 2:, late], acc_late[:])
-
-        def scaled(dst, t, cols, src):
-            nc.vector.tensor_tensor(dst, scale_rows[t][:].indirect(entries(task_sb, cols)), src, MULT)
-
+        y = sb.tile([P, PACK, S], F32, name="y", align_bytes=64)
+        picked0 = sb.tile([P, S], F32, name="picked0", align_bytes=64)
+        picked1 = sb.tile([P, HALF], F32, name="picked1", align_bytes=64)
+        held1 = sb.tile([P, HALF], F32, name="held1", align_bytes=64)
+        held2 = turns.tile([P, HALF], F32, name="held2", offset=0)
+        held3 = sb.tile([P, HALF], F32, name="held3", align_bytes=64)
+        picked2 = sb.tile([P, HALF], F32, name="picked2", align_bytes=64)
+        picked3 = sb.tile([P, HALF], F32, name="picked3", align_bytes=64)
         out_dealt = out_0.rearrange("(p t) s -> p t s", t=PACK)
-        rest = second
-        picked0 = prod[:, 0, rest]
-        nc.vector.tensor_copy(picked0, scale_rows[0][:].indirect(entries(task_sb, rest)))
+
+        def look_up(t, cols):
+            return scale_rows[t][:].indirect(entries(task_sb, cols))
+
+        acc1a = product(1, first)
+        acc0a = product(0, first)
+        acc3a = product(3, first)
+        acc2a = product(2, first)
+        acc0b = product(0, second)
+        acc1b = product(1, second)
+        acc2b = product(2, second)
+        acc3b = product(3, second)
+
+        for cols in (first, second):
+            nc.scalar.activation(picked0[:, cols], look_up(0, cols), COPY)
+        nc.scalar.copy(held2[:], acc2a[:])
+        nc.scalar.activation(picked1[:], look_up(1, second), COPY)
+        nc.vector.tensor_copy(held1[:], acc1a[:])
+        nc.vector.tensor_tensor(y[:, 0, first], acc0a[:], picked0[:, first], MULT)
+        nc.vector.tensor_tensor(y[:, 1, first], look_up(1, first), held1[:], MULT)
+        nc.vector.tensor_tensor(y[:, 0, second], acc0b[:], picked0[:, second], MULT)
+        nc.vector.tensor_copy(held3[:], acc3a[:])
+        nc.vector.tensor_tensor(y[:, 1, second], acc1b[:], picked1[:], MULT)
+        nc.sync.dma_start(out_dealt[:, :2, :], y[:, :2, :])
+        nc.scalar.activation(picked2[:], look_up(2, second), COPY)
+        nc.vector.tensor_tensor(y[:, 2, first], look_up(2, first), held2[:], MULT)
+        nc.vector.tensor_tensor(y[:, 2, second], acc2b[:], picked2[:], MULT)
+        nc.sync.dma_start(out_dealt[:, 2, :], y[:, 2, :])
         for cols in quarters[:2]:
-            scaled(y_early[:, 0, cols], 0, cols, prod[:, 0, cols])
-        scaled(y_early[:, 1, first], 1, first, parked1)
-        scaled(y_early[:, 1, third], 1, third, prod[:, 1, third])
-        scaled(y_late[:, 1, :], 1, late, prod[:, 1, late])
-        nc.sync.dma_start(out_dealt[:, 1, late], y_late[:, 1, :])
-        nc.vector.tensor_tensor(y[:, rest], acc0[:], picked0, MULT)
-        nc.sync.dma_start(out_0.rearrange("(p t) s -> p (t s)", t=PACK)[:, : S + EARLY], y[:, : S + EARLY])
-        scaled(y_early[:, 2, :], 2, early, prod[:, 2, early])
-        nc.sync.dma_start(out_dealt[:, 2, early], y_early[:, 2, :])
-        scaled(y_early[:, 3, :HEAD], 3, slice(0, HEAD), parked3)
-        for cols in (slice(HEAD, 192), slice(192, EARLY)):
-            scaled(y_early[:, 3, cols], 3, cols, prod[:, 3, cols])
-        nc.sync.dma_start(out_dealt[:, 3, early], y_early[:, 3, :])
-        for t in (2, 3):
-            scaled(y_late[:, t, :], t, late, prod[:, t, late])
-        nc.sync.dma_start(out_dealt[:, 2:, late], y_late[:, 2:, :])
+            nc.scalar.activation(picked3[:, cols], look_up(3, slice(cols.start + HALF, cols.stop + HALF)), COPY)
+        for cols in quarters[:2]:
+            nc.vector.tensor_tensor(y[:, 3, cols], look_up(3, cols), held3[:, cols], MULT)
+        for cols in quarters[:2]:
+            nc.vector.tensor_tensor(y[:, 3, cols.start + HALF : cols.stop + HALF], acc3b[:, cols], picked3[:, cols], MULT)
+        nc.sync.dma_start(out_dealt[:, 3, :], y[:, 3, :])
 
         y_codes = sb.tile([P, S], I32, name="y_codes", align_bytes=64)
         y_scales = sb.tile([P, S], U8, name="y_scales", align_bytes=64)
         words_out = out_1[0].rearrange("p c r -> p (c r)").bitcast(I32)
         y_bf = sb.tile([P, S, PACK], BF16, name="y_bf", align_bytes=64)
 
-        def rounded(copy, cols, src):
-            copy(y_bf[:, cols].rearrange("p (c i) t -> p c t i", i=4), src.rearrange("p t (c i) -> p c t i", i=4))
+        def rounded(copy, cols):
+            copy(
+                y_bf[:, cols].rearrange("p (c i) t -> p c t i", i=4),
+                y[:, :, cols].rearrange("p t (c i) -> p c t i", i=4),
+            )
 
         def quantised(cols):
             nc.vector.quantize_mx(
@@ -172,17 +167,15 @@ def tile_picked_none_po_kernel(
                 scales=y_scales[:, cols],
                 in_=y_bf[:, cols].rearrange("p c t -> p (c t)"),
             )
+            nc.sync.dma_start(words_out[:, cols], y_codes[:, cols])
 
-        for cols in (slice(0, HEAD), slice(HEAD, 192), slice(192, HALF), slice(HALF, HALF + THIRD_SHARE)):
-            rounded(nc.scalar.copy, cols, y_early[:, :, cols])
-        rounded(nc.scalar.copy, slice(EARLY, EARLY + SHARE), y_late[:, :, :SHARE])
-        rounded(nc.vector.tensor_copy, slice(HALF + THIRD_SHARE, EARLY), y_early[:, :, HALF + THIRD_SHARE :])
-        rounded(nc.vector.tensor_copy, slice(EARLY + SHARE, S), y_late[:, :, SHARE:])
-        quantised(first)
-        nc.sync.dma_start(words_out[:, first], y_codes[:, first])
-        quantised(third)
-        quantised(late)
-        nc.sync.dma_start(words_out[:, second], y_codes[:, second])
+        for cols in quarters[:2]:
+            rounded(nc.scalar.copy, cols)
+        for cols in quarters[2:]:
+            rounded(nc.vector.tensor_copy, cols)
+        quantised(quarters[0])
+        quantised(second)
+        quantised(quarters[1])
         ys_rows = out_2[0].rearrange("(q r) c -> r q c", r=4)
         for r in range(4):
             eng = nc.sync if r % 2 else nc.scalar

@@ -146,9 +146,10 @@ def tile_picked_none_po_kernel(
             nc.scalar.activation(picked3[:, cols], look_up(3, slice(cols.start + HALF, cols.stop + HALF)), COPY)
         for cols in quarters[:2]:
             nc.vector.tensor_tensor(y[:, 3, cols], look_up(3, cols), held3[:, cols], MULT)
+        nc.sync.dma_start(out_dealt[:, 3, first], y[:, 3, first])
         for cols in quarters[:2]:
             nc.vector.tensor_tensor(y[:, 3, cols.start + HALF : cols.stop + HALF], acc3b[:, cols], picked3[:, cols], MULT)
-        nc.sync.dma_start(out_dealt[:, 3, :], y[:, 3, :])
+        nc.sync.dma_start(out_dealt[:, 3, second], y[:, 3, second])
 
         y_codes = sb.tile([P, S], I32, name="y_codes", align_bytes=64)
         y_scales = sb.tile([P, S], U8, name="y_scales", align_bytes=64)

@@ -135,9 +135,10 @@ def tile_picked_none_po_kernel(
         nc.vector.tensor_tensor(y[:, 0, first], acc0a[:], picked0[:, first], MULT)
         nc.vector.tensor_tensor(y[:, 1, first], look_up(1, first), held1[:], MULT)
         nc.vector.tensor_tensor(y[:, 0, second], acc0b[:], picked0[:, second], MULT)
+        nc.sync.dma_start(out_dealt[:, 0, :], y[:, 0, :])
         nc.vector.tensor_copy(held3[:], acc3a[:])
         nc.vector.tensor_tensor(y[:, 1, second], acc1b[:], picked1[:], MULT)
-        nc.sync.dma_start(out_dealt[:, :2, :], y[:, :2, :])
+        nc.sync.dma_start(out_dealt[:, 1, :], y[:, 1, :])
         nc.scalar.activation(picked2[:], look_up(2, second), COPY)
         nc.vector.tensor_tensor(y[:, 2, first], look_up(2, first), held2[:], MULT)
         nc.vector.tensor_tensor(y[:, 2, second], acc2b[:], picked2[:], MULT)

@@ -147,10 +147,9 @@ def tile_picked_none_po_kernel(
             nc.scalar.activation(picked3[:, cols], look_up(3, slice(cols.start + HALF, cols.stop + HALF)), COPY)
         for cols in quarters[:2]:
             nc.vector.tensor_tensor(y[:, 3, cols], look_up(3, cols), held3[:, cols], MULT)
-        nc.sync.dma_start(out_dealt[:, 3, first], y[:, 3, first])
         for cols in quarters[:2]:
             nc.vector.tensor_tensor(y[:, 3, cols.start + HALF : cols.stop + HALF], acc3b[:, cols], picked3[:, cols], MULT)
-        nc.sync.dma_start(out_dealt[:, 3, second], y[:, 3, second])
+        nc.sync.dma_start(out_dealt[:, 3, :], y[:, 3, :])
 
         y_codes = sb.tile([P, S], I32, name="y_codes", align_bytes=64)
         y_scales = sb.tile([P, S], U8, name="y_scales", align_bytes=64)
@@ -169,15 +168,18 @@ def tile_picked_none_po_kernel(
                 scales=y_scales[:, cols],
                 in_=y_bf[:, cols].rearrange("p c t -> p (c t)"),
             )
-            nc.sync.dma_start(words_out[:, cols], y_codes[:, cols])
 
         for cols in quarters[:2]:
             rounded(nc.scalar.copy, cols)
         for cols in quarters[2:]:
             rounded(nc.vector.tensor_copy, cols)
         quantised(quarters[0])
-        quantised(second)
+        nc.sync.dma_start(words_out[:, quarters[0]], y_codes[:, quarters[0]])
+        quantised(quarters[2])
+        quantised(quarters[3])
+        nc.sync.dma_start(words_out[:, second], y_codes[:, second])
         quantised(quarters[1])
+        nc.sync.dma_start(words_out[:, quarters[1]], y_codes[:, quarters[1]])
         ys_rows = out_2[0].rearrange("(q r) c -> r q c", r=4)
         for r in range(4):
             eng = nc.sync if r % 2 else nc.scalar

@@ -84,9 +84,8 @@ def tile_picked_none_po_kernel(
         first, second = slice(0, HALF), slice(HALF, S)
 
         x_picked = sb.tile([P, S], U32, name="x_picked", align_bytes=64)
-        for cols in (first, second):
+        for cols in (quarters[0], quarters[1], second):
             nc.vector.tensor_copy(x_picked[:, cols], x_table[:].bitcast(U32).indirect(entries(offs_sb, cols)))
-
 
         def matmul(dst, t, cols):
             wc = slice(t * P, (t + 1) * P)
@@ -106,49 +105,48 @@ def tile_picked_none_po_kernel(
             return acc
 
         y = sb.tile([P, PACK, S], F32, name="y", align_bytes=64)
-        picked0 = sb.tile([P, S], F32, name="picked0", align_bytes=64)
-        picked1 = sb.tile([P, HALF], F32, name="picked1", align_bytes=64)
-        held1 = sb.tile([P, HALF], F32, name="held1", align_bytes=64)
-        held2 = turns.tile([P, HALF], F32, name="held2", offset=0)
-        held3 = sb.tile([P, HALF], F32, name="held3", align_bytes=64)
-        picked2 = sb.tile([P, HALF], F32, name="picked2", align_bytes=64)
-        picked3 = sb.tile([P, HALF], F32, name="picked3", align_bytes=64)
+        parked = {1: sb.tile([P, HALF], F32, name="parked1", align_bytes=64)}
+        for t in (2, 3):
+            parked[t] = turns.tile([P, HALF], F32, name=f"parked{t}", offset=(t - 2) * 4 * HALF)
+        picked = [sb.tile([P, HALF], F32, name=f"picked{t}", align_bytes=64) for t in range(PACK)]
         out_dealt = out_0.rearrange("(p t) s -> p t s", t=PACK)
 
         def look_up(t, cols):
             return scale_rows[t][:].indirect(entries(task_sb, cols))
 
-        acc1a = product(1, first)
-        acc0a = product(0, first)
-        acc3a = product(3, first)
-        acc2a = product(2, first)
-        acc0b = product(0, second)
-        acc1b = product(1, second)
-        acc2b = product(2, second)
-        acc3b = product(3, second)
+        early1 = psum.tile([P, HALF], F32, name="early1")
+        for cols in quarters[:2]:
+            matmul(early1[:, cols], 1, cols)
+        early0 = product(0, first)
+        early2 = product(2, first)
+        late = [product(t, second) for t in (0, 1)]
+        early3 = product(3, first)
+        late = late + [product(t, second) for t in (2, 3)]
 
-        for cols in (first, second):
-            nc.scalar.activation(picked0[:, cols], look_up(0, cols), COPY)
-        nc.scalar.copy(held2[:], acc2a[:])
-        nc.scalar.activation(picked1[:], look_up(1, second), COPY)
-        nc.vector.tensor_copy(held1[:], acc1a[:])
-        nc.vector.tensor_tensor(y[:, 0, first], acc0a[:], picked0[:, first], MULT)
-        nc.vector.tensor_tensor(y[:, 1, first], look_up(1, first), held1[:], MULT)
-        nc.vector.tensor_tensor(y[:, 0, second], acc0b[:], picked0[:, second], MULT)
+        picked_q1 = sb.tile([P, QUARTER], F32, name="picked_q1", align_bytes=64)
+        early_picked = (y[:, 1, quarters[0]], picked_q1[:])
+        nc.vector.tensor_copy(parked[1][:], early1[:])
+        for cols, place in zip(quarters, early_picked):
+            nc.scalar.activation(place, look_up(0, cols), COPY)
+        nc.scalar.activation(picked[0][:], look_up(0, second), COPY)
+        for cols, place in zip(quarters, early_picked):
+            nc.vector.tensor_tensor(y[:, 0, cols], early0[:, cols], place, MULT)
+        nc.vector.tensor_tensor(y[:, 1, first], look_up(1, first), parked[1][:], MULT)
+        nc.vector.tensor_tensor(y[:, 0, second], late[0][:], picked[0][:], MULT)
         nc.sync.dma_start(out_dealt[:, 0, :], y[:, 0, :])
-        nc.vector.tensor_copy(held3[:], acc3a[:])
-        nc.vector.tensor_tensor(y[:, 1, second], acc1b[:], picked1[:], MULT)
-        nc.sync.dma_start(out_dealt[:, 1, :], y[:, 1, :])
-        nc.scalar.activation(picked2[:], look_up(2, second), COPY)
-        nc.vector.tensor_tensor(y[:, 2, first], look_up(2, first), held2[:], MULT)
-        nc.vector.tensor_tensor(y[:, 2, second], acc2b[:], picked2[:], MULT)
-        nc.sync.dma_start(out_dealt[:, 2, :], y[:, 2, :])
+        for t, acc in ((1, early2), (2, early3)):
+            nc.scalar.activation(picked[t][:], look_up(t, second), COPY)
+            nc.scalar.copy(parked[t + 1][:], acc[:])
+            if t == 2:
+                nc.vector.tensor_tensor(y[:, t, first], look_up(t, first), parked[t][:], MULT)
+            nc.vector.tensor_tensor(y[:, t, second], late[t][:], picked[t][:], MULT)
+            nc.sync.dma_start(out_dealt[:, t, :], y[:, t, :])
         for cols in quarters[:2]:
-            nc.scalar.activation(picked3[:, cols], look_up(3, slice(cols.start + HALF, cols.stop + HALF)), COPY)
+            nc.scalar.activation(picked[3][:, cols], look_up(3, slice(cols.start + HALF, cols.stop + HALF)), COPY)
         for cols in quarters[:2]:
-            nc.vector.tensor_tensor(y[:, 3, cols], look_up(3, cols), held3[:, cols], MULT)
+            nc.vector.tensor_tensor(y[:, 3, cols], look_up(3, cols), parked[3][:, cols], MULT)
         for cols in quarters[:2]:
-            nc.vector.tensor_tensor(y[:, 3, cols.start + HALF : cols.stop + HALF], acc3b[:, cols], picked3[:, cols], MULT)
+            nc.vector.tensor_tensor(y[:, 3, cols.start + HALF : cols.stop + HALF], late[3][:, cols], picked[3][:, cols], MULT)
         nc.sync.dma_start(out_dealt[:, 3, :], y[:, 3, :])
 
         y_codes = sb.tile([P, S], I32, name="y_codes", align_bytes=64)

@@ -34,6 +34,7 @@ def tile_picked_none_po_kernel(
         offs_sb = lists.tile([P, S // PER_COL], U16, name="offs_sb")
         task_sb = lists.tile([P, S // PER_COL], U16, name="task_sb")
         turns = ctx.enter_context(tc.tile_pool(name="turns", bufs=1))
+        again = ctx.enter_context(tc.tile_pool(name="again", bufs=1))
         row_bytes = 4 * U
         w_raw = sb.tile([P, PACK, N], F32, name="w_raw")
         xs_room = turns.tile([P, 2 * row_bytes + 64], U8, name="xs_room", offset=row_bytes - 32)
@@ -108,7 +109,7 @@ def tile_picked_none_po_kernel(
         parked = {1: sb.tile([P, HALF], F32, name="parked1", align_bytes=64)}
         for t in (2, 3):
             parked[t] = turns.tile([P, HALF], F32, name=f"parked{t}", offset=(t - 2) * 4 * HALF)
-        picked = [sb.tile([P, HALF], F32, name=f"picked{t}", align_bytes=64) for t in range(PACK)]
+        picked = [sb.tile([P, HALF], F32, name=f"picked{t}", align_bytes=64) for t in range(3)]
         out_dealt = out_0.rearrange("(p t) s -> p t s", t=PACK)
 
         def look_up(t, cols):
@@ -141,22 +142,29 @@ def tile_picked_none_po_kernel(
                 nc.vector.tensor_tensor(y[:, t, first], look_up(t, first), parked[t][:], MULT)
             nc.vector.tensor_tensor(y[:, t, second], late[t][:], picked[t][:], MULT)
             nc.sync.dma_start(out_dealt[:, t, :], y[:, t, :])
-        for cols in quarters[:2]:
-            nc.scalar.activation(picked[3][:, cols], look_up(3, slice(cols.start + HALF, cols.stop + HALF)), COPY)
+        last_picked = [
+            again.tile([P, QUARTER], F32, name="picked_q2", offset=0, align_bytes=64),
+            sb.tile([P, QUARTER], F32, name="picked_q3", align_bytes=64),
+        ]
+        for cols, place in zip(quarters[2:], last_picked):
+            nc.scalar.activation(place[:], look_up(3, cols), COPY)
         for cols in quarters[:2]:
             nc.vector.tensor_tensor(y[:, 3, cols], look_up(3, cols), parked[3][:, cols], MULT)
-        for cols in quarters[:2]:
-            nc.vector.tensor_tensor(y[:, 3, cols.start + HALF : cols.stop + HALF], late[3][:, cols], picked[3][:, cols], MULT)
+        for cols, place in zip(quarters[:2], last_picked):
+            nc.vector.tensor_tensor(y[:, 3, cols.start + HALF : cols.stop + HALF], late[3][:, cols], place[:], MULT)
         nc.sync.dma_start(out_dealt[:, 3, :], y[:, 3, :])
 
         y_codes = sb.tile([P, S], I32, name="y_codes", align_bytes=64)
         y_scales = sb.tile([P, S], U8, name="y_scales", align_bytes=64)
         words_out = out_1[0].rearrange("p c r -> p (c r)").bitcast(I32)
-        y_bf = sb.tile([P, S, PACK], BF16, name="y_bf", align_bytes=64)
+        y_bf = {
+            cols.start: again.tile([P, QUARTER, PACK], BF16, name=f"y_bf{q}", offset=1024 * ((q - 1) % 4), align_bytes=64)
+            for q, cols in enumerate(quarters)
+        }
 
         def rounded(copy, cols):
             copy(
-                y_bf[:, cols].rearrange("p (c i) t -> p c t i", i=4),
+                y_bf[cols.start][:].rearrange("p (c i) t -> p c t i", i=4),
                 y[:, :, cols].rearrange("p t (c i) -> p c t i", i=4),
             )
 
@@ -164,20 +172,19 @@ def tile_picked_none_po_kernel(
             nc.vector.quantize_mx(
                 out=y_codes[:, cols].bitcast(FP8X4),
                 scales=y_scales[:, cols],
-                in_=y_bf[:, cols].rearrange("p c t -> p (c t)"),
+                in_=y_bf[cols.start][:].rearrange("p c t -> p (c t)"),
             )
 
+        rounded(nc.scalar.copy, quarters[0])
+        rounded(nc.vector.tensor_copy, quarters[1])
+        rounded(nc.vector.tensor_copy, quarters[2])
+        rounded(nc.scalar.copy, quarters[3])
         for cols in quarters[:2]:
-            rounded(nc.scalar.copy, cols)
+            quantised(cols)
+            nc.sync.dma_start(words_out[:, cols], y_codes[:, cols])
         for cols in quarters[2:]:
-            rounded(nc.vector.tensor_copy, cols)
-        quantised(quarters[0])
-        nc.sync.dma_start(words_out[:, quarters[0]], y_codes[:, quarters[0]])
-        quantised(quarters[2])
-        quantised(quarters[3])
+            quantised(cols)
         nc.sync.dma_start(words_out[:, second], y_codes[:, second])
-        quantised(quarters[1])
-        nc.sync.dma_start(words_out[:, quarters[1]], y_codes[:, quarters[1]])
         ys_rows = out_2[0].rearrange("(q r) c -> r q c", r=4)
         for r in range(4):
             eng = nc.sync if r % 2 else nc.scalar

@@ -132,16 +132,23 @@ def tile_picked_none_po_kernel(
         nc.scalar.activation(picked[0][:], look_up(0, second), COPY)
         for cols, place in zip(quarters, early_picked):
             nc.vector.tensor_tensor(y[:, 0, cols], early0[:, cols], place, MULT)
+        out_runs = out_0.rearrange("(p t) s -> p (t s)", t=PACK)
+        y_runs = y[:].rearrange("p t s -> p (t s)")
+        nc.sync.dma_start(out_runs[:, first], y_runs[:, first])
         nc.vector.tensor_tensor(y[:, 1, first], look_up(1, first), parked[1][:], MULT)
         nc.vector.tensor_tensor(y[:, 0, second], late[0][:], picked[0][:], MULT)
-        nc.sync.dma_start(out_dealt[:, 0, :], y[:, 0, :])
-        for t, acc in ((1, early2), (2, early3)):
-            nc.scalar.activation(picked[t][:], look_up(t, second), COPY)
-            nc.scalar.copy(parked[t + 1][:], acc[:])
-            if t == 2:
-                nc.vector.tensor_tensor(y[:, t, first], look_up(t, first), parked[t][:], MULT)
-            nc.vector.tensor_tensor(y[:, t, second], late[t][:], picked[t][:], MULT)
-            nc.sync.dma_start(out_dealt[:, t, :], y[:, t, :])
+        nc.scalar.activation(picked[1][:], look_up(1, second), COPY)
+        nc.scalar.copy(parked[2][:], early2[:])
+        nc.vector.tensor_tensor(y[:, 1, second], late[1][:], picked[1][:], MULT)
+        nc.sync.dma_start(out_runs[:, HALF : 2 * S], y_runs[:, HALF : 2 * S])
+        for cols, there in zip(quarters[2:], quarters):
+            nc.scalar.activation(picked[2][:, there], look_up(2, cols), COPY)
+        for cols in quarters[:2]:
+            nc.scalar.copy(parked[3][:, cols], early3[:, cols])
+        nc.vector.tensor_tensor(y[:, 2, first], look_up(2, first), parked[2][:], MULT)
+        for cols, there in zip(quarters[2:], quarters):
+            nc.vector.tensor_tensor(y[:, 2, cols], late[2][:, there], picked[2][:, there], MULT)
+        nc.sync.dma_start(out_dealt[:, 2, :], y[:, 2, :])
         last_picked = [
             again.tile([P, QUARTER], F32, name="picked_q2", offset=0, align_bytes=64),
             sb.tile([P, QUARTER], F32, name="picked_q3", align_bytes=64),

@@ -50,16 +50,18 @@ def tile_picked_none_po_kernel(
         nc.sync.dma_start(w_raw[:, :1], w_dealt[:, :1])
         nc.sync.dma_start(offs_sb[:], offs)
         nc.sync.dma_start(task_sb[:], task)
-        nc.sync.dma_start(xs_room[0:16, :T].bitcast(I32), x_scales[0].bitcast(I32))
+        nc.sync.dma_start(xs_room[64:80, :T].bitcast(I32), x_scales[0].bitcast(I32))
         nc.sync.dma_start(w_raw[:, 1:], w_dealt[:, 1:])
         nc.sync.dma_start(x_table[:], x_rows)
         scale_dealt = scale.rearrange("(p t) u -> p t u", t=PACK)
         scale_rows = []
 
         nc.vector.tensor_copy(xs_picked[:], xs_table.indirect(offs_sb[:]))
-        for q in range(1, 4):
-            nc.sync.dma_start(xs_placed[32 * q : 32 * q + 4, :].bitcast(I32), xs_picked[4 * q : 4 * q + 4, :].bitcast(I32))
-        nc.vector.tensor_copy(xs_placed[:32, :].bitcast(I32), xs_picked[:32, :].bitcast(I32))
+        for q in (0, 1, 3):
+            nc.sync.dma_start(
+                xs_placed[32 * q + 8 : 32 * q + 12, :].bitcast(I32), xs_picked[64 + 4 * q : 68 + 4 * q, :].bitcast(I32)
+            )
+        nc.vector.tensor_copy(xs_placed[64:96, :].bitcast(I32), xs_picked[64:96, :].bitcast(I32))
 
         w_bf = sb.tile([P, PACK, P, PACK], BF16, name="w_bf", align_bytes=64)
         w_src = w_raw[:].rearrange("p j (m u e) -> p u m j e", u=2, e=2)
@@ -95,7 +97,7 @@ def tile_picked_none_po_kernel(
                 lhsT=w_codes[:, wc].bitcast(FP8X4),
                 lhsT_scale=w_scales[:, wc],
                 rhs=x_picked[:, cols].bitcast(FP8X4),
-                rhs_scale=xs_placed[:, cols],
+                rhs_scale=xs_placed[8:, cols],
                 start=True,
                 stop=True,
             )

from contextlib import ExitStack

import concourse.mybir as mybir

K, T, S, N, U = 512, 2048, 512, 512, 1024
FLOPS = 2 * K * N * S

F32 = mybir.dt.float32
BF16 = mybir.dt.bfloat16
I32 = mybir.dt.int32
U32 = mybir.dt.uint32
U16 = mybir.dt.uint16
U8 = mybir.dt.uint8
FP8X4 = mybir.dt.float8_e4m3fn_x4
MULT = mybir.AluOpType.mult
COPY = mybir.ActivationFunctionType.Copy

P = 128
PACK = 4
HALF = S // 2
QUARTER = S // 4
PER_COL = 16


def tile_picked_none_po_kernel(
    tc, x_words, x_scales, w1, scale, offs, task, out_0, out_1, out_2
):
    nc = tc.nc
    with ExitStack() as ctx:
        lists = ctx.enter_context(tc.tile_pool(name="lists", bufs=1))
        sb = ctx.enter_context(tc.tile_pool(name="sb", bufs=1))
        psum = ctx.enter_context(tc.psum_pool(name="psum", bufs=1))

        offs_sb = lists.tile([P, S // PER_COL], U16, name="offs_sb")
        task_sb = lists.tile([P, S // PER_COL], U16, name="task_sb")
        turns = ctx.enter_context(tc.tile_pool(name="turns", bufs=1))
        again = ctx.enter_context(tc.tile_pool(name="again", bufs=1))
        row_bytes = 4 * U
        w_raw = sb.tile([P, PACK, N], F32, name="w_raw")
        xs_room = turns.tile([P, 2 * row_bytes + 64], U8, name="xs_room", offset=row_bytes - 32)
        xs_table = xs_room[:, :T]
        x_table = sb.tile([P, T], I32, name="x_table", align_bytes=64)
        xs_picked = sb.tile([P, S], U8, name="xs_picked", align_bytes=64)
        xs_placed = sb.tile([P, S], U8, name="xs_placed", align_bytes=64)

        nc.vector.memset(xs_table.bitcast(I32), 0)
        nc.vector.memset(xs_placed[:].bitcast(I32), 0)
        x_rows = x_words[0].rearrange("p c r -> p (c r)").bitcast(I32)
        w_dealt = w1.rearrange("(p j) m -> p j m", j=PACK)
        nc.sync.dma_start(w_raw[:, :1], w_dealt[:, :1])
        nc.sync.dma_start(offs_sb[:], offs)
        nc.sync.dma_start(task_sb[:], task)
        nc.sync.dma_start(xs_room[64:80, :T].bitcast(I32), x_scales[0].bitcast(I32))
        nc.sync.dma_start(w_raw[:, 1:], w_dealt[:, 1:])
        nc.sync.dma_start(x_table[:], x_rows)
        scale_dealt = scale.rearrange("(p t) u -> p t u", t=PACK)
        scale_rows = []

        nc.vector.tensor_copy(xs_picked[:], xs_table.indirect(offs_sb[:]))
        for q in (0, 1, 3):
            nc.sync.dma_start(
                xs_placed[32 * q + 8 : 32 * q + 12, :].bitcast(I32), xs_picked[64 + 4 * q : 68 + 4 * q, :].bitcast(I32)
            )
        nc.vector.tensor_copy(xs_placed[64:96, :].bitcast(I32), xs_picked[64:96, :].bitcast(I32))

        w_bf = sb.tile([P, PACK, P, PACK], BF16, name="w_bf", align_bytes=64)
        w_src = w_raw[:].rearrange("p j (m u e) -> p u m j e", u=2, e=2)
        w_dst = w_bf[:].rearrange("p (u e) m j -> p u m j e", u=2)
        for u in range(2):
            nc.vector.tensor_copy(w_dst[:, u], w_src[:, u])
        for t in range(PACK):
            scale_rows.append(turns.tile([P, U], F32, name=f"scale_rows{t}", offset=t * row_bytes))
            nc.sync.dma_start(scale_rows[t][:], scale_dealt[:, t, :])
        w_codes = sb.tile([P, N], U32, name="w_codes", align_bytes=64)
        w_scales = sb.tile([P, N], U8, name="w_scales", align_bytes=64)
        for u in range(2):
            nc.vector.quantize_mx(
                out=w_codes[:, 2 * u * P : 2 * (u + 1) * P].bitcast(FP8X4),
                scales=w_scales[:, 2 * u * P : 2 * (u + 1) * P],
                in_=w_bf[:, 2 * u : 2 * u + 2].rearrange("p t m j -> p (t m j)"),
            )

        def entries(lst, cols):
            return lst[:, cols.start // PER_COL : cols.stop // PER_COL]

        quarters = [slice(q * QUARTER, (q + 1) * QUARTER) for q in range(4)]
        first, second = slice(0, HALF), slice(HALF, S)

        x_picked = sb.tile([P, S], U32, name="x_picked", align_bytes=64)
        for cols in (quarters[0], quarters[1], second):
            nc.vector.tensor_copy(x_picked[:, cols], x_table[:].bitcast(U32).indirect(entries(offs_sb, cols)))

        def matmul(dst, t, cols):
            wc = slice(t * P, (t + 1) * P)
            nc.tensor.matmul_mx(
                out=dst,
                lhsT=w_codes[:, wc].bitcast(FP8X4),
                lhsT_scale=w_scales[:, wc],
                rhs=x_picked[:, cols].bitcast(FP8X4),
                rhs_scale=xs_placed[8:, cols],
                start=True,
                stop=True,
            )

        def product(t, cols):
            acc = psum.tile([P, cols.stop - cols.start], F32, name=f"acc{t}_{cols.start}")
            matmul(acc[:], t, cols)
            return acc

        y = sb.tile([P, PACK, S], F32, name="y", align_bytes=64)
        parked = {1: sb.tile([P, HALF], F32, name="parked1", align_bytes=64)}
        for t in (2, 3):
            parked[t] = turns.tile([P, HALF], F32, name=f"parked{t}", offset=(t - 2) * 4 * HALF)
        picked = [sb.tile([P, HALF], F32, name=f"picked{t}", align_bytes=64) for t in range(3)]
        out_dealt = out_0.rearrange("(p t) s -> p t s", t=PACK)

        def look_up(t, cols):
            return scale_rows[t][:].indirect(entries(task_sb, cols))

        early1 = psum.tile([P, HALF], F32, name="early1")
        for cols in quarters[:2]:
            matmul(early1[:, cols], 1, cols)
        early0 = product(0, first)
        early2 = product(2, first)
        late = [product(t, second) for t in (0, 1)]
        early3 = product(3, first)
        late = late + [product(t, second) for t in (2, 3)]

        picked_q1 = sb.tile([P, QUARTER], F32, name="picked_q1", align_bytes=64)
        early_picked = (y[:, 1, quarters[0]], picked_q1[:])
        nc.vector.tensor_copy(parked[1][:], early1[:])
        for cols, place in zip(quarters, early_picked):
            nc.scalar.activation(place, look_up(0, cols), COPY)
        nc.scalar.activation(picked[0][:], look_up(0, second), COPY)
        for cols, place in zip(quarters, early_picked):
            nc.vector.tensor_tensor(y[:, 0, cols], early0[:, cols], place, MULT)
        out_runs = out_0.rearrange("(p t) s -> p (t s)", t=PACK)
        y_runs = y[:].rearrange("p t s -> p (t s)")
        nc.sync.dma_start(out_runs[:, first], y_runs[:, first])
        nc.vector.tensor_tensor(y[:, 1, first], look_up(1, first), parked[1][:], MULT)
        nc.vector.tensor_tensor(y[:, 0, second], late[0][:], picked[0][:], MULT)
        nc.scalar.activation(picked[1][:], look_up(1, second), COPY)
        nc.scalar.copy(parked[2][:], early2[:])
        nc.vector.tensor_tensor(y[:, 1, second], late[1][:], picked[1][:], MULT)
        nc.sync.dma_start(out_runs[:, HALF : 2 * S], y_runs[:, HALF : 2 * S])
        for cols, there in zip(quarters[2:], quarters):
            nc.scalar.activation(picked[2][:, there], look_up(2, cols), COPY)
        for cols in quarters[:2]:
            nc.scalar.copy(parked[3][:, cols], early3[:, cols])
        nc.vector.tensor_tensor(y[:, 2, first], look_up(2, first), parked[2][:], MULT)
        for cols, there in zip(quarters[2:], quarters):
            nc.vector.tensor_tensor(y[:, 2, cols], late[2][:, there], picked[2][:, there], MULT)
        nc.sync.dma_start(out_dealt[:, 2, :], y[:, 2, :])
        last_picked = [
            again.tile([P, QUARTER], F32, name="picked_q2", offset=0, align_bytes=64),
            sb.tile([P, QUARTER], F32, name="picked_q3", align_bytes=64),
        ]
        for cols, place in zip(quarters[2:], last_picked):
            nc.scalar.activation(place[:], look_up(3, cols), COPY)
        for cols in quarters[:2]:
            nc.vector.tensor_tensor(y[:, 3, cols], look_up(3, cols), parked[3][:, cols], MULT)
        for cols, place in zip(quarters[:2], last_picked):
            nc.vector.tensor_tensor(y[:, 3, cols.start + HALF : cols.stop + HALF], late[3][:, cols], place[:], MULT)
        nc.sync.dma_start(out_dealt[:, 3, :], y[:, 3, :])

        y_codes = sb.tile([P, S], I32, name="y_codes", align_bytes=64)
        y_scales = sb.tile([P, S], U8, name="y_scales", align_bytes=64)
        words_out = out_1[0].rearrange("p c r -> p (c r)").bitcast(I32)
        y_bf = {
            cols.start: again.tile([P, QUARTER, PACK], BF16, name=f"y_bf{q}", offset=1024 * ((q - 1) % 4), align_bytes=64)
            for q, cols in enumerate(quarters)
        }

        def rounded(copy, cols):
            copy(
                y_bf[cols.start][:].rearrange("p (c i) t -> p c t i", i=4),
                y[:, :, cols].rearrange("p t (c i) -> p c t i", i=4),
            )

        def quantised(cols):
            nc.vector.quantize_mx(
                out=y_codes[:, cols].bitcast(FP8X4),
                scales=y_scales[:, cols],
                in_=y_bf[cols.start][:].rearrange("p c t -> p (c t)"),
            )

        rounded(nc.scalar.copy, quarters[0])
        rounded(nc.vector.tensor_copy, quarters[1])
        rounded(nc.vector.tensor_copy, quarters[2])
        rounded(nc.scalar.copy, quarters[3])
        for cols in quarters[:2]:
            quantised(cols)
            nc.sync.dma_start(words_out[:, cols], y_codes[:, cols])
        for cols in quarters[2:]:
            quantised(cols)
        nc.sync.dma_start(words_out[:, second], y_codes[:, second])
        ys_rows = out_2[0].rearrange("(q r) c -> r q c", r=4)
        for r in range(4):
            eng = nc.sync if r % 2 else nc.scalar
            eng.dma_start(ys_rows[r].bitcast(I32), y_scales[r:P:32, :].bitcast(I32))
